import numpy as np
import ml_dtypes


def mxq(x, axis, fmt="e4m3"):
    dtype, down = {"e4m3": (ml_dtypes.float8_e4m3fn, 7), "e5m2": (ml_dtypes.float8_e5m2, 14)}[fmt]
    v = np.moveaxis(np.asarray(x, np.float32).astype(ml_dtypes.bfloat16).astype(np.float64), axis, -1)
    blocks = v.reshape(v.shape[:-1] + (-1, 32))
    amax = np.abs(blocks).max(-1, keepdims=True)
    byte = np.maximum(np.where(amax > 0, np.frexp(amax)[1] - 1 + 127, 0) - down, 1)
    scale = np.exp2(byte - 127.0)
    codes = (blocks / scale).astype(np.float32).astype(dtype).astype(np.float64)
    return np.moveaxis((codes * scale).reshape(v.shape), -1, axis)


WIDE = False


def mx_kscale(k):
    if not WIDE:
        return np.ones(k)
    levels = np.array([10, -10, 5, -5, 0])
    if k % 512:
        return np.exp2(np.random.permutation(np.resize(levels, k // 32))).repeat(32)
    a = np.empty((k // 512, 16))
    for p in range(k // 512):
        a[p, :8] = np.random.permutation(np.resize(levels, 8))
        for g in range(8):
            far = levels[np.abs(levels - a[p, g]) >= 10]
            a[p, g + 8] = far[np.random.randint(len(far))]
    return np.exp2(a.ravel()).repeat(32)


BF16 = ml_dtypes.bfloat16


def bf(x):
    return np.asarray(x, np.float32).astype(BF16)


def f64(x):
    return np.asarray(x).astype(np.float64)


E2M1 = np.array([0.0, 0.5, 1.0, 1.5, 2.0, 3.0, 4.0, 6.0, -0.0, -0.5, -1.0, -1.5, -2.0, -3.0, -4.0, -6.0])


def pack_weight(w, fmt):
    k, n = w.shape
    w = f64(bf(w)).reshape(k // 32, 32, n)
    amax = np.abs(w).max(1)
    if fmt == "e4m3":
        byte = np.frexp(amax)[1] - 1 + 127 - 7
    else:
        mant, ex = np.frexp(amax / 6.0)
        byte = np.where(mant > 0.5, ex, ex - 1) + 127
    byte = np.clip(np.where(amax > 0, byte, 1), 1, 254)
    scaled = (w * np.exp2(127.0 - byte)[:, None, :]).reshape(k, n).astype(np.float32)
    by_word = np.ascontiguousarray(scaled.reshape(k // 512, 128, 4, n).transpose(0, 1, 3, 2))
    if fmt == "e4m3":
        words = by_word.astype(ml_dtypes.float8_e4m3fn).view(np.uint8)
    else:
        c = by_word.astype(ml_dtypes.float4_e2m1fn).view(np.uint8) & 0xF
        words = c[..., 0::2] | (c[..., 1::2] << 4)
    return np.ascontiguousarray(words), np.ascontiguousarray(byte.astype(np.uint8).reshape(k // 512, 16, n))


def unpack_weight(words, scales, fmt):
    g, p, n, _ = words.shape
    if fmt == "e4m3":
        vals = np.ascontiguousarray(words).view(ml_dtypes.float8_e4m3fn).astype(np.float64)
    else:
        nib = np.empty((g, p, n, 4), np.uint8)
        nib[..., 0::2] = words & 0xF
        nib[..., 1::2] = words >> 4
        vals = E2M1[nib]
    vals = vals * np.repeat(np.exp2(scales.astype(np.float64) - 127.0), 8, axis=1)[..., None]
    return vals.transpose(0, 1, 3, 2).reshape(g * 512, n)
def pack4(w):
    words, scales = pack_weight(w, "e2m1")
    return words.reshape(words.shape[0], 128, -1), scales


def unpack4(words, scales):
    return unpack_weight(words.reshape(words.shape[0], 128, -1, 2), scales, "e2m1")


E4M3FN = np.array([(-1.0 if i & 128 else 1.0) * ((1.0 + (i & 7) / 8.0) * 2.0 ** (((i >> 3) & 15) - 7) if i & 120 else (i & 7) * 2.0 ** -9) for i in range(256)])


def e4m3fn_bytes(y):
    return np.clip(np.asarray(y, np.float64), -448.0, 448.0).astype(np.float32).astype(ml_dtypes.float8_e4m3fn).view(np.uint8)


def e4m3fn_values(b):
    return E4M3FN[b]

def planes(Y):
    n, m = Y.shape
    b = f64(bf(Y)).reshape(n // 32, 32, m)
    amax = np.abs(b).max(1)
    byte = np.clip(np.where(amax > 0, np.frexp(amax)[1] - 1 + 127 - 7, 1), 1, 254)
    codes = (b * np.exp2(127.0 - byte)[:, None, :]).reshape(n, m).astype(np.float32).astype(ml_dtypes.float8_e4m3fn).view(np.uint8)
    words = codes.reshape(n // 512, 128, 4, m).transpose(0, 1, 3, 2)
    return np.ascontiguousarray(words), np.ascontiguousarray(byte.astype(np.uint8).reshape(n // 512, 16, m))


T, D, F, BL = 768, 1536, 1024, 128
FP8_MAX = 448.0
KICK = 0.4
DRIFT = 0.35


def setup_inputs():
    s = mx_kscale(D)
    t = mx_kscale(F)
    x = np.random.randn(T, D) * s
    d = np.random.randn(T, F)
    A = KICK * np.random.randn(D, F) / np.sqrt(D) / s[:, None]
    A_scale = (np.abs(A).reshape(D // BL, BL, F // BL, BL).max(axis=(1, 3)) / FP8_MAX).astype(np.float32)
    A_bytes = e4m3fn_bytes(A / np.repeat(np.repeat(f64(A_scale), BL, axis=0), BL, axis=1))
    B = DRIFT * np.random.randn(F, D) / np.sqrt(F) * s[None, :] / t[:, None]
    B_words, B_scales = pack4(B)
    C = KICK * np.random.randn(D, F) / np.sqrt(D) / s[:, None]
    stride = np.exp(0.4 * np.random.randn(1, F)) * t
    gain = np.exp(0.8 * np.random.randn(1, F))
    return {"x": bf(x), "d": bf(d), "A_bytes": A_bytes, "A_scale": A_scale,
            "B_words": B_words, "B_scales": B_scales, "C": bf(C),
            "stride": bf(stride), "gain": bf(gain)}


def reference(x, d, A_bytes, A_scale, B_words, B_scales, C, stride, gain):
    x, d, C, stride, gain = f64(x), f64(d), f64(C), f64(stride), f64(gain)
    A = e4m3fn_values(A_bytes) * np.repeat(np.repeat(f64(A_scale), BL, axis=0), BL, axis=1)
    e = d + (mxq(x, 1) @ mxq(A, 0))
    u = e * stride
    x1 = x + (mxq(u, 1) @ unpack4(B_words, B_scales))
    y = (e + (mxq(x1, 1) @ mxq(C, 0))) * gain
    words, scales = planes(y.T)
    return y, words, scales

@@ -1,0 +1,410 @@
+from contextlib import ExitStack
+
+import concourse.mybir as mybir
+from concourse.masks import make_identity
+
+T, D, F = 768, 1536, 1024
+FLOPS = 2 * T * D * F * 3
+
+F32 = mybir.dt.float32
+BF16 = mybir.dt.bfloat16
+U32 = mybir.dt.uint32
+I32 = mybir.dt.int32
+U8 = mybir.dt.uint8
+FP8 = mybir.dt.float8_e4m3fn
+FP8X4 = mybir.dt.float8_e4m3fn_x4
+FP4X4 = mybir.dt.float4_e2m1fn_x4
+ALU = mybir.AluOpType
+COPY = mybir.ActivationFunctionType.Copy
+
+P = 128
+PACK = 4
+KP = P * PACK
+GD = D // KP
+GF = F // KP
+PAIR = 2 * P
+PAIRS = T // PAIR
+BLK = 128
+
+
+def tile_linear_leapfrog_difference_b9_kernel(
+    tc, x, d, A_bytes, A_scale, B_words, B_scales, C, stride, gain, out_0, out_1, out_2
+):
+    nc = tc.nc
+    with ExitStack() as ctx:
+        keep = ctx.enter_context(tc.tile_pool(name="keep", bufs=1))
+        work = ctx.enter_context(tc.tile_pool(name="work", bufs=3))
+        psum = ctx.enter_context(tc.psum_pool(name="psum", bufs=4))
+
+        def kept(name, shape, dtype):
+            return keep.tile(shape, dtype, name=name, align_bytes=64)
+
+        def staged(name, shape, dtype, bufs):
+            return work.tile(shape, dtype, name=name, tag=name, bufs=bufs, align_bytes=64)
+
+        def bank(role):
+            return psum.tile([P, KP], F32, name=role, tag=role)
+
+        def quantize(codes, scales, values):
+            nc.vector.quantize_mx(out=codes.bitcast(FP8X4), scales=scales, in_=values)
+
+        ident = kept("ident", [P, P], F32)
+        make_identity(nc, ident[:])
+        b_scale = kept("b_scale", [P, GF, D], U8)
+        nc.gpsimd.memset(b_scale[:].rearrange("p g n -> p (g n)").bitcast(I32), 0)
+
+        ctx.enter_context(tc.manual_schedule())
+        a_scale_all = kept("a_scale_all", [P, (D // BLK) * (F // BLK)], F32)
+        a_raw, c_raw, x_sb, d_sb = {}, {}, {}, {}
+
+        def load_a(h, g):
+            a_raw[h, g] = kept("a_bytes_%d_%d" % (h, g), [P, PACK, KP], U8)
+            rows = A_bytes[g * KP : (g + 1) * KP, h * KP : (h + 1) * KP]
+            nc.sync.dma_start(out=a_raw[h, g][:], in_=rows.rearrange("(p j) f -> p j f", j=PACK))
+
+        def load_c(h, g):
+            c_raw[h, g] = kept("c_raw_%d_%d" % (h, g), [P, PACK, KP], BF16)
+            rows = C[g * KP : (g + 1) * KP, h * KP : (h + 1) * KP]
+            nc.sync.dma_start(out=c_raw[h, g][:], in_=rows.rearrange("(p j) f -> p j f", j=PACK))
+
+        def load_x(q):
+            x_sb[q] = kept("x_%d" % q, [P, 2, D], BF16)
+            rows = x[q * PAIR : (q + 1) * PAIR, :]
+            nc.sync.dma_start(out=x_sb[q][:], in_=rows.rearrange("(i p) k -> p i k", p=P))
+
+        def load_d(q):
+            d_sb[q] = kept("d_%d" % q, [P, 2, F], BF16)
+            rows = d[q * PAIR : (q + 1) * PAIR, :]
+            nc.sync.dma_start(out=d_sb[q][:], in_=rows.rearrange("(i p) f -> p i f", p=P))
+
+        def load_cols():
+            nc.sync.dma_start(out=stride_raw[:], in_=stride.rearrange("o (g p t) -> p (o g) t", p=P, t=PACK))
+            nc.sync.dma_start(out=gain_raw[:], in_=gain.rearrange("o (g p t) -> p (o g) t", p=P, t=PACK))
+
+        def load_b():
+            for quad in range(4):
+                nc.sync.dma_start(
+                    out=b_scale[32 * quad : 32 * quad + 4, :, :].bitcast(I32),
+                    in_=B_scales[:, 4 * quad : 4 * quad + 4, :].rearrange("g r n -> r g n").bitcast(I32),
+                )
+            nc.sync.dma_start(
+                out=b_words[:].bitcast(I32), in_=B_words.rearrange("g p n -> p g n").bitcast(I32)
+            )
+
+        stride_raw = kept("stride_raw", [P, GF, PACK], BF16)
+        gain_raw = kept("gain_raw", [P, GF, PACK], BF16)
+        b_words = kept("b_words", [P, GF, 2 * D], U8)
+        nc.sync.dma_start(
+            out=a_scale_all[:], in_=A_scale.rearrange("a b -> (a b)").partition_broadcast(P)
+        )
+        load_a(0, 0)
+        load_a(0, 1)
+        load_x(0)
+        load_a(0, 2)
+        load_x(1)
+        load_a(1, 0)
+        load_d(0)
+        load_a(1, 1)
+        load_cols()
+        load_a(1, 2)
+        load_d(1)
+        load_x(2)
+        load_c(0, 0)
+        load_b()
+        load_d(2)
+        load_c(0, 1)
+        load_c(0, 2)
+        for g in range(GD):
+            load_c(1, g)
+
+        a_scale = kept("a_scale", [P, GD, F // BLK], F32)
+        by_row = a_scale_all[:].rearrange("p (g q b) -> p g q b", g=GD, q=4)
+        for quad in range(4):
+            part = slice(32 * quad, 32 * quad + 32)
+            nc.scalar.activation(out=a_scale[part], in_=by_row[part, :, quad, :], func=COPY)
+        stride_col = kept("stride_col", [P, GF, PACK], F32)
+        gain_col = kept("gain_col", [P, GF, PACK], F32)
+
+        a_codes, a_scales, c_codes, c_scales = {}, {}, {}, {}
+        x_codes, x_scales, u_codes, u_scales = {}, {}, {}, {}
+        x1_codes, x1_scales = {}, {}
+        eg = {}
+        y_scales = kept("y_scales", [P, GF, T], U8)
+        words_out = out_1.rearrange("g p m t -> g p (m t)").bitcast(I32)
+
+        def copy_on(engine, out, in_):
+            if engine == "V":
+                nc.vector.tensor_copy(out=out, in_=in_)
+            else:
+                nc.scalar.copy(out=out, in_=in_)
+
+        def quantized(name, codes, scales, key, grouped, bufs):
+            width = grouped.shape[1] // PACK
+            codes[key] = staged(name + "_codes", [P, width], U32, bufs)
+            scales[key] = staged(name + "_scales", [P, width], U8, bufs)
+            quantize(codes[key][:], scales[key][:], grouped)
+
+        def unit_cols():
+            def group():
+                nc.vector.tensor_copy(out=stride_col[:], in_=stride_raw[:])
+                nc.vector.tensor_copy(out=gain_col[:], in_=gain_raw[:])
+            return {"group": group}
+
+        def unit_a(h, g, engine):
+            st = {}
+
+            def widen():
+                st["wide"] = staged("a_wide", [P, PACK, KP], BF16, 2)
+                copy_on(
+                    engine,
+                    st["wide"][:].rearrange("p j f -> p (j f)"),
+                    a_raw[h, g][:].rearrange("p j f -> p (j f)").bitcast(FP8),
+                )
+
+            def group():
+                st["grouped"] = staged("w_grouped", [P, PACK, P, PACK], BF16, 3)
+                src = st["wide"][:].rearrange("p j (m t) -> p t m j", t=PACK)
+                for b in range(KP // BLK):
+                    ms = slice(32 * b, 32 * b + 32)
+                    col = h * (KP // BLK) + b
+                    nc.vector.tensor_scalar(
+                        out=st["grouped"][:, :, ms, :], in0=src[:, :, ms, :],
+                        scalar1=a_scale[:, g, col : col + 1], scalar2=None, op0=ALU.mult,
+                    )
+
+            def quant():
+                quantized("a", a_codes, a_scales, (h, g), st["grouped"][:].rearrange("p t m j -> p (t m j)"), 6)
+
+            return {"drain": widen, "group": group, "quant": quant}
+
+        def unit_c(h, g, engine):
+            st = {}
+
+            def group():
+                st["grouped"] = staged("w_grouped", [P, PACK, P, PACK], BF16, 3)
+                copy_on(
+                    engine,
+                    st["grouped"][:].rearrange("p t (n m) j -> p n t m j", m=2),
+                    c_raw[h, g][:].rearrange("p j (n m t) -> p n t m j", m=2, t=PACK),
+                )
+
+            def quant():
+                quantized("c", c_codes, c_scales, (h, g), st["grouped"][:].rearrange("p t m j -> p (t m j)"), 6)
+
+            return {"group" if engine == "V" else "drain": group, "quant": quant}
+
+        def turn_words(st, source):
+            st["ps"] = bank("turn")
+            halves = st["ps"][:].rearrange("p (i u r) -> p i u r", i=2, u=2)
+            for i in range(2):
+                for u in range(2):
+                    nc.tensor.transpose(halves[:, i, u, :], source(i, u), ident[:])
+
+        def drain_words(st):
+            st["grouped"] = staged("pos_grouped", [P, PAIR * PACK], BF16, 4)
+            nc.scalar.copy(
+                out=st["grouped"][:].bitcast(F32).rearrange("p (i r u) -> p i r u", i=2, u=2),
+                in_=st["ps"][:].rearrange("p (i u r) -> p i r u", i=2, u=2),
+            )
+
+        def unit_x(q, g):
+            st = {}
+            words = x_sb[q][:].bitcast(F32)
+            return {
+                "turn": lambda: turn_words(st, lambda i, u: words[:, i, 256 * g + u : 256 * (g + 1) : 2]),
+                "drain": lambda: drain_words(st),
+                "quant": lambda: quantized("x", x_codes, x_scales, (q, g), st["grouped"][:], 9),
+            }
+
+        def unit_kick(q, h):
+            st = {}
+
+            def matmul():
+                st["sums"] = []
+                for i in range(2):
+                    ps = bank("sum")
+                    st["sums"].append(ps)
+                    cols = slice(i * P, (i + 1) * P)
+                    for g in range(GD):
+                        nc.tensor.matmul_mx(
+                            out=ps[:],
+                            lhsT=x_codes[q, g][:, cols].bitcast(FP8X4), lhsT_scale=x_scales[q, g][:, cols],
+                            rhs=a_codes[h, g][:].bitcast(FP8X4), rhs_scale=a_scales[h, g][:],
+                            start=(g == 0), stop=(g == GD - 1),
+                        )
+
+            def add():
+                st["e"] = staged("e", [P, 2, KP], F32, 2)
+                for i in range(2):
+                    nc.vector.tensor_tensor(
+                        out=st["e"][:, i, :].rearrange("p (t m) -> p t m", t=PACK),
+                        in0=st["sums"][i][:].rearrange("p (t m) -> p t m", t=PACK),
+                        in1=d_sb[q][:, i, h * KP : (h + 1) * KP].rearrange("p (m t) -> p t m", t=PACK),
+                        op=ALU.add,
+                    )
+
+            def turn():
+                st["turned"] = []
+                for half in range(2):
+                    ps = bank("turn")
+                    st["turned"].append(ps)
+                    for s in range(2):
+                        t = 2 * half + s
+                        for i in range(2):
+                            nc.tensor.transpose(
+                                ps[:, s * PAIR + i * P : s * PAIR + (i + 1) * P],
+                                st["e"][:, i, t * P : (t + 1) * P], ident[:],
+                            )
+
+            def scaled(dst, col):
+                for t in range(PACK):
+                    nc.scalar.activation(
+                        out=dst[:, t, :], in_=st["turned"][t // 2][:, (t % 2) * PAIR : (t % 2 + 1) * PAIR],
+                        func=COPY, scale=col[:, h, t : t + 1],
+                    )
+
+            def drain():
+                st["planes"] = staged("u_planes", [P, PACK, PAIR], BF16, 2)
+                scaled(st["planes"], stride_col)
+
+            def save():
+                eg[q, h] = kept("eg_%d_%d" % (q, h), [P, PACK, PAIR], F32)
+                scaled(eg[q, h], gain_col)
+
+            def group():
+                st["grouped"] = staged("mode_grouped", [P, PAIR, PACK], BF16, 3)
+                nc.vector.tensor_copy(out=st["grouped"][:], in_=st["planes"][:].rearrange("p t r -> p r t"))
+
+            def quant():
+                quantized("u", u_codes, u_scales, (q, h), st["grouped"][:].rearrange("p r t -> p (r t)"), 6)
+
+            return {"matmul": matmul, "add": add, "turn": turn, "drain": drain, "save": save, "group": group, "quant": quant}
+
+        def unit_drift(q, g):
+            st = {}
+
+            def matmul():
+                st["sums"] = []
+                for i in range(2):
+                    ps = bank("sum")
+                    st["sums"].append(ps)
+                    cols = slice(i * P, (i + 1) * P)
+                    for h in range(GF):
+                        nc.tensor.matmul_mx(
+                            out=ps[:],
+                            lhsT=u_codes[q, h][:, cols].bitcast(FP8X4), lhsT_scale=u_scales[q, h][:, cols],
+                            rhs=b_words[:, h, 2 * KP * g : 2 * KP * (g + 1)].bitcast(FP4X4),
+                            rhs_scale=b_scale[:, h, KP * g : KP * (g + 1)],
+                            start=(h == 0), stop=(h == GF - 1),
+                        )
+
+            def add():
+                st["x1"] = staged("x1", [P, 2, KP], BF16, 2)
+                for i in range(2):
+                    nc.vector.tensor_tensor(
+                        out=st["x1"][:, i, :].rearrange("p (u m e) -> p u m e", u=2, e=2),
+                        in0=st["sums"][i][:].rearrange("p (m u e) -> p u m e", u=2, e=2),
+                        in1=x_sb[q][:, i, g * KP : (g + 1) * KP].rearrange("p (m u e) -> p u m e", u=2, e=2),
+                        op=ALU.add,
+                    )
+
+            return {
+                "matmul": matmul,
+                "add": add,
+                "turn": lambda: turn_words(st, lambda i, u: st["x1"][:].bitcast(F32)[:, i, u * P : (u + 1) * P]),
+                "drain": lambda: drain_words(st),
+                "quant": lambda: quantized("x1", x1_codes, x1_scales, (q, g), st["grouped"][:], 9),
+            }
+
+        def unit_kick2(q, h, engine):
+            st = {}
+            cols = slice(q * PAIR, (q + 1) * PAIR)
+
+            def matmul():
+                st["sums"] = []
+                for half in range(2):
+                    ps = bank("sum")
+                    st["sums"].append(ps)
+                    for s in range(2):
+                        t = 2 * half + s
+                        for g in range(GD):
+                            nc.tensor.matmul_mx(
+                                out=ps[:, s * PAIR : (s + 1) * PAIR],
+                                lhsT=c_codes[h, g][:, t * P : (t + 1) * P].bitcast(FP8X4),
+                                lhsT_scale=c_scales[h, g][:, t * P : (t + 1) * P],
+                                rhs=x1_codes[q, g][:].bitcast(FP8X4), rhs_scale=x1_scales[q, g][:],
+                                start=(g == 0), stop=(g == GD - 1),
+                            )
+
+            def add():
+                st["y"] = staged("y_turned", [P, PACK, PAIR], F32, 3)
+                for t in range(PACK):
+                    nc.vector.scalar_tensor_tensor(
+                        out=st["y"][:, t, :], in0=st["sums"][t // 2][:, (t % 2) * PAIR : (t % 2 + 1) * PAIR],
+                        scalar=gain_col[:, h, t : t + 1], in1=eg[q, h][:, t, :],
+                        op0=ALU.mult, op1=ALU.add,
+                    )
+
+            def turn():
+                st["turned"] = []
+                for i in range(2):
+                    ps = bank("turn")
+                    st["turned"].append(ps)
+                    for t in range(PACK):
+                        nc.tensor.transpose(
+                            ps[:, t * P : (t + 1) * P], st["y"][:, t, i * P : (i + 1) * P], ident[:]
+                        )
+
+            def drain():
+                if engine == "S":
+                    group()
+                for i in range(2):
+                    y = staged("y", [P, P, PACK], F32, 4)
+                    nc.scalar.copy(out=y[:], in_=st["turned"][i][:].rearrange("r (t m) -> r m t", t=PACK))
+                    rows = slice(q * PAIR + i * P, q * PAIR + (i + 1) * P)
+                    nc.sync.dma_start(
+                        out=out_0[rows, h * KP : (h + 1) * KP], in_=y[:].rearrange("r m t -> r (m t)")
+                    )
+
+            def group():
+                st["grouped"] = staged("mode_grouped", [P, PAIR, PACK], BF16, 3)
+                copy_on(engine, st["grouped"][:], st["y"][:].rearrange("p t r -> p r t"))
+
+            def quant():
+                y_codes = staged("y_codes", [P, PAIR], U32, 4)
+                quantize(y_codes[:], y_scales[:, h, cols], st["grouped"][:].rearrange("p r t -> p (r t)"))
+                nc.sync.dma_start(out=words_out[h, :, cols], in_=y_codes[:].bitcast(I32))
+
+            stages = {"matmul": matmul, "add": add, "turn": turn, "drain": drain, "quant": quant}
+            if engine == "V":
+                stages["group"] = group
+            return stages
+
+        units = {"cols": unit_cols()}
+        for g in range(GD):
+            for h in range(GF):
+                units["A%d%d" % (h, g)] = unit_a(h, g, "VSSVSS"[h * GD + g])
+                units["C%d%d" % (h, g)] = unit_c(h, g, "SSSSSS"[h * GD + g])
+            for q in range(PAIRS):
+                units["X%d%d" % (q, g)] = unit_x(q, g)
+                units["D%d%d" % (q, g)] = unit_drift(q, g)
+        for q in range(PAIRS):
+            for h in range(GF):
+                units["K%d%d" % (q, h)] = unit_kick(q, h)
+                units["Y%d%d" % (q, h)] = unit_kick2(q, h, "VVVVVV"[q * GF + h])
+        steps = []
+
+        def run(stage, step):
+            if 0 <= step < len(steps):
+                for unit in steps[step]:
+                    if stage in unit:
+                        unit[stage]()
+
+        for name, stage in [("A00", "drain"), ("A01", "drain"), ("A02", "drain"), ("A00", "group"), ("A01", "group"), ("A00", "quant"), ("A01", "quant"), ("X00", "turn"), ("X01", "turn"), ("X02", "turn"), ("X00", "drain"), ("X01", "drain"), ("X02", "drain"), ("A02", "group"), ("A10", "drain"), ("A02", "quant"), ("X00", "quant"), ("X01", "quant"), ("X02", "quant"), ("X10", "turn"), ("X11", "turn"), ("X12", "turn"), ("K00", "matmul"), ("X10", "drain"), ("X11", "drain"), ("X12", "drain"), ("A11", "drain"), ("A10", "group"), ("X10", "quant"), ("X11", "quant"), ("X12", "quant"), ("K10", "matmul"), ("cols", "group"), ("K00", "add"), ("A10", "quant"), ("K00", "turn"), ("A12", "drain"), ("A11", "group"), ("K10", "add"), ("X20", "turn"), ("X21", "turn"), ("X22", "turn"), ("A11", "quant"), ("K00", "drain"), ("K00", "save"), ("K10", "turn"), ("A12", "group"), ("K00", "group"), ("A12", "quant"), ("K01", "matmul"), ("K11", "matmul"), ("K00", "quant"), ("X20", "drain"), ("X21", "drain"), ("X22", "drain"), ("K10", "drain"), ("K10", "save"), ("C00", "drain"), ("X20", "quant"), ("X21", "quant"), ("X22", "quant"), ("K01", "add"), ("K10", "group"), ("K01", "turn"), ("K20", "matmul"), ("K11", "add"), ("K10", "quant"), ("K01", "drain"), ("K01", "save"), ("K11", "turn"), ("K20", "add"), ("C00", "quant"), ("K21", "matmul"), ("K01", "group"), ("K11", "drain"), ("K11", "save"), ("K01", "quant"), ("K20", "turn"), ("D00", "matmul"), ("K21", "add"), ("K11", "group"), ("K20", "drain"), ("K20", "save"), ("D01", "matmul"), ("D00", "add"), ("K11", "quant"), ("K21", "turn"), ("D02", "matmul"), ("D00", "turn"), ("D01", "add"), ("K20", "group"), ("D00", "drain"), ("K21", "drain"), ("K21", "save"), ("C01", "drain"), ("D10", "matmul"), ("D02", "add"), ("K20", "quant"), ("D01", "turn"), ("D01", "drain"), ("D11", "matmul"), ("D10", "add"), ("D00", "quant"), ("D02", "turn"), ("D02", "drain"), ("C02", "drain"), ("K21", "group"), ("D12", "matmul"), ("D11", "add"), ("D01", "quant"), ("D10", "turn"), ("K21", "quant"), ("C01", "quant"), ("D20", "matmul"), ("D12", "add"), ("D02", "quant"), ("C02", "quant"), ("D10", "drain"), ("D11", "turn"), ("D11", "drain"), ("C10", "drain"), ("Y00", "matmul"), ("D20", "add"), ("D10", "quant"), ("D12", "turn"), ("D12", "drain"), ("D21", "matmul"), ("Y00", "add"), ("D11", "quant"), ("D20", "turn"), ("C10", "quant"), ("D20", "drain"), ("C11", "drain"), ("D22", "matmul"), ("D21", "add"), ("D12", "quant"), ("Y00", "turn"), ("Y00", "group"), ("Y10", "matmul"), ("D22", "add"), ("D20", "quant"), ("D21", "turn"), ("D21", "drain"), ("Y00", "quant"), ("C11", "quant"), ("D22", "turn"), ("D22", "drain"), ("C12", "drain"), ("Y00", "drain"), ("Y10", "add"), ("D21", "quant"), ("D22", "quant"), ("Y20", "matmul"), ("Y10", "group"), ("C12", "quant"), ("Y10", "turn"), ("Y10", "drain"), ("Y01", "matmul"), ("Y20", "add"), ("Y10", "quant"), ("Y20", "turn"), ("Y20", "drain"), ("Y11", "matmul"), ("Y20", "group"), ("Y01", "add"), ("Y20", "quant"), ("Y01", "turn"), ("Y01", "drain"), ("Y21", "matmul"), ("Y01", "group"), ("Y11", "add"), ("Y01", "quant"), ("Y11", "turn"), ("Y11", "drain"), ("Y11", "group"), ("Y21", "add"), ("Y11", "quant"), ("Y21", "turn"), ("Y21", "group"), ("Y21", "drain"), ("Y21", "quant")]:
+            units[name][stage]()
+
+        for quad in range(4):
+            nc.sync.dma_start(
+                out=out_2[:, 4 * quad : 4 * quad + 4, :].rearrange("g r m -> r g m").bitcast(I32),
+                in_=y_scales[32 * quad : 32 * quad + 4, :, :].bitcast(I32),
+            )

@@ -25,6 +25,7 @@ GF = F // KP
 PAIR = 2 * P
 PAIRS = T // PAIR
 BLK = 128
+BLOCKS = (D // BLK) * (F // BLK)
 
 
 def tile_linear_leapfrog_difference_b9_kernel(
@@ -49,12 +50,13 @@ def tile_linear_leapfrog_difference_b9_kernel(
             nc.vector.quantize_mx(out=codes.bitcast(FP8X4), scales=scales, in_=values)
 
         ident = kept("ident", [P, P], F32)
-        make_identity(nc, ident[:])
         b_scale = kept("b_scale", [P, GF, D], U8)
-        nc.gpsimd.memset(b_scale[:].rearrange("p g n -> p (g n)").bitcast(I32), 0)
 
-        ctx.enter_context(tc.manual_schedule())
-        a_scale_all = kept("a_scale_all", [P, (D // BLK) * (F // BLK)], F32)
+        ctx.enter_context(tc.manual_schedule(engines={mybir.EngineType.PE, mybir.EngineType.SP}))
+        a_scale_flat = kept("a_scale_flat", [P, 1], F32)
+        nc.gpsimd.memset(a_scale_flat[BLOCKS:P, :], 0.0)
+        make_identity(nc, ident[:])
+        nc.gpsimd.memset(b_scale[:].rearrange("p g n -> p (g n)").bitcast(I32), 0)
         a_raw, c_raw, x_sb, d_sb = {}, {}, {}, {}
 
         def load_a(h, g):
@@ -62,10 +64,10 @@ def tile_linear_leapfrog_difference_b9_kernel(
             rows = A_bytes[g * KP : (g + 1) * KP, h * KP : (h + 1) * KP]
             nc.sync.dma_start(out=a_raw[h, g][:], in_=rows.rearrange("(p j) f -> p j f", j=PACK))
 
-        def load_c(h, g):
-            c_raw[h, g] = kept("c_raw_%d_%d" % (h, g), [P, PACK, KP], BF16)
-            rows = C[g * KP : (g + 1) * KP, h * KP : (h + 1) * KP]
-            nc.sync.dma_start(out=c_raw[h, g][:], in_=rows.rearrange("(p j) f -> p j f", j=PACK))
+        def load_c(g):
+            c_raw[g] = kept("c_raw_%d" % g, [P, PACK, F], BF16)
+            rows = C[g * KP : (g + 1) * KP, :]
+            nc.sync.dma_start(out=c_raw[g][:], in_=rows.rearrange("(p j) f -> p j f", j=PACK))
 
         def load_x(q):
             x_sb[q] = kept("x_%d" % q, [P, 2, D], BF16)
@@ -94,31 +96,31 @@ def tile_linear_leapfrog_difference_b9_kernel(
         stride_raw = kept("stride_raw", [P, GF, PACK], BF16)
         gain_raw = kept("gain_raw", [P, GF, PACK], BF16)
         b_words = kept("b_words", [P, GF, 2 * D], U8)
-        nc.sync.dma_start(
-            out=a_scale_all[:], in_=A_scale.rearrange("a b -> (a b)").partition_broadcast(P)
-        )
+        scale_rows = A_scale.rearrange("a (b o) -> (a b) o", o=1)
+        nc.sync.dma_start(out=a_scale_flat[0:64, :], in_=scale_rows[0:64, :])
+        nc.sync.dma_start(out=a_scale_flat[64:BLOCKS, :], in_=scale_rows[64:BLOCKS, :])
         load_a(0, 0)
         load_a(0, 1)
         load_x(0)
         load_a(0, 2)
+        load_d(0)
+        load_cols()
         load_x(1)
         load_a(1, 0)
-        load_d(0)
-        load_a(1, 1)
-        load_cols()
-        load_a(1, 2)
         load_d(1)
+        load_a(1, 1)
         load_x(2)
-        load_c(0, 0)
-        load_b()
+        load_a(1, 2)
         load_d(2)
-        load_c(0, 1)
-        load_c(0, 2)
-        for g in range(GD):
-            load_c(1, g)
+        load_c(0)
+        load_b()
+        load_c(1)
+        load_c(2)
 
         a_scale = kept("a_scale", [P, GD, F // BLK], F32)
-        by_row = a_scale_all[:].rearrange("p (g q b) -> p g q b", g=GD, q=4)
+        spread = bank("sum")
+        nc.tensor.transpose(spread[:, 0:P], a_scale_flat[:].to_broadcast([P, P]), ident[:])
+        by_row = spread[:, 0:BLOCKS].rearrange("p (g q b) -> p g q b", g=GD, q=4)
         for quad in range(4):
             part = slice(32 * quad, 32 * quad + 32)
             nc.scalar.activation(out=a_scale[part], in_=by_row[part, :, quad, :], func=COPY)
@@ -128,7 +130,8 @@ def tile_linear_leapfrog_difference_b9_kernel(
         a_codes, a_scales, c_codes, c_scales = {}, {}, {}, {}
         x_codes, x_scales, u_codes, u_scales = {}, {}, {}, {}
         x1_codes, x1_scales = {}, {}
-        eg = {}
+        d_turned = {}
+        e = [kept("e_%d" % h, [P, PACK, T], F32) for h in range(GF)]
         y_scales = kept("y_scales", [P, GF, T], U8)
         words_out = out_1.rearrange("g p m t -> g p (m t)").bitcast(I32)
 
@@ -137,6 +140,13 @@ def tile_linear_leapfrog_difference_b9_kernel(
                 nc.vector.tensor_copy(out=out, in_=in_)
             else:
                 nc.scalar.copy(out=out, in_=in_)
+
+        def interleave(engine, grouped, planes):
+            copy_on(
+                engine,
+                grouped[:].rearrange("p (c i) t -> p c t i", i=PACK),
+                planes[:].rearrange("p t (c i) -> p c t i", i=PACK),
+            )
 
         def quantized(name, codes, scales, key, grouped, bufs):
             width = grouped.shape[1] // PACK
@@ -163,12 +173,13 @@ def tile_linear_leapfrog_difference_b9_kernel(
 
             def group():
                 st["grouped"] = staged("w_grouped", [P, PACK, P, PACK], BF16, 3)
-                src = st["wide"][:].rearrange("p j (m t) -> p t m j", t=PACK)
+                src = st["wide"][:].rearrange("p j (m t) -> p m j t", t=PACK)
+                dst = st["grouped"][:].rearrange("p t m j -> p m j t")
                 for b in range(KP // BLK):
                     ms = slice(32 * b, 32 * b + 32)
                     col = h * (KP // BLK) + b
                     nc.vector.tensor_scalar(
-                        out=st["grouped"][:, :, ms, :], in0=src[:, :, ms, :],
+                        out=dst[:, ms], in0=src[:, ms],
                         scalar1=a_scale[:, g, col : col + 1], scalar2=None, op0=ALU.mult,
                     )
 
@@ -184,8 +195,8 @@ def tile_linear_leapfrog_difference_b9_kernel(
                 st["grouped"] = staged("w_grouped", [P, PACK, P, PACK], BF16, 3)
                 copy_on(
                     engine,
-                    st["grouped"][:].rearrange("p t (n m) j -> p n t m j", m=2),
-                    c_raw[h, g][:].rearrange("p j (n m t) -> p n t m j", m=2, t=PACK),
+                    st["grouped"][:].rearrange("p t m j -> p m j t"),
+                    c_raw[g][:, :, h * KP : (h + 1) * KP].rearrange("p j (m t) -> p m j t", t=PACK),
                 )
 
             def quant():
@@ -216,69 +227,84 @@ def tile_linear_leapfrog_difference_b9_kernel(
                 "quant": lambda: quantized("x", x_codes, x_scales, (q, g), st["grouped"][:], 9),
             }
 
-        def unit_kick(q, h):
+        def unit_d(q, h):
             st = {}
-
-            def matmul():
-                st["sums"] = []
-                for i in range(2):
-                    ps = bank("sum")
-                    st["sums"].append(ps)
-                    cols = slice(i * P, (i + 1) * P)
-                    for g in range(GD):
-                        nc.tensor.matmul_mx(
-                            out=ps[:],
-                            lhsT=x_codes[q, g][:, cols].bitcast(FP8X4), lhsT_scale=x_scales[q, g][:, cols],
-                            rhs=a_codes[h, g][:].bitcast(FP8X4), rhs_scale=a_scales[h, g][:],
-                            start=(g == 0), stop=(g == GD - 1),
-                        )
-
-            def add():
-                st["e"] = staged("e", [P, 2, KP], F32, 2)
-                for i in range(2):
-                    nc.vector.tensor_tensor(
-                        out=st["e"][:, i, :].rearrange("p (t m) -> p t m", t=PACK),
-                        in0=st["sums"][i][:].rearrange("p (t m) -> p t m", t=PACK),
-                        in1=d_sb[q][:, i, h * KP : (h + 1) * KP].rearrange("p (m t) -> p t m", t=PACK),
-                        op=ALU.add,
-                    )
+            words = d_sb[q][:].bitcast(F32)
 
             def turn():
-                st["turned"] = []
-                for half in range(2):
-                    ps = bank("turn")
-                    st["turned"].append(ps)
-                    for s in range(2):
-                        t = 2 * half + s
-                        for i in range(2):
-                            nc.tensor.transpose(
-                                ps[:, s * PAIR + i * P : s * PAIR + (i + 1) * P],
-                                st["e"][:, i, t * P : (t + 1) * P], ident[:],
-                            )
+                st["ps"] = bank("turn")
+                halves = st["ps"][:].rearrange("p (u i r) -> p u i r", i=2, u=2)
+                for u in range(2):
+                    for i in range(2):
+                        nc.tensor.transpose(
+                            halves[:, u, i, :], words[:, i, 256 * h + u : 256 * (h + 1) : 2], ident[:]
+                        )
 
-            def scaled(dst, col):
+            def drain():
+                d_turned[q, h] = staged("d_turned", [P, KP], F32, 4)
+                nc.scalar.copy(out=d_turned[q, h][:], in_=st["ps"][:])
+
+            return {"turn": turn, "drain": drain}
+
+        def weights_stationary(codes, scales, h, moving_codes, moving_scales, q):
+            sums = []
+            for half in range(2):
+                ps = bank("sum")
+                sums.append(ps)
+                for s in range(2):
+                    t = 2 * half + s
+                    for g in range(GD):
+                        nc.tensor.matmul_mx(
+                            out=ps[:, s * PAIR : (s + 1) * PAIR],
+                            lhsT=codes[h, g][:, t * P : (t + 1) * P].bitcast(FP8X4),
+                            lhsT_scale=scales[h, g][:, t * P : (t + 1) * P],
+                            rhs=moving_codes[q, g][:].bitcast(FP8X4), rhs_scale=moving_scales[q, g][:],
+                            start=(g == 0), stop=(g == GD - 1),
+                        )
+            return sums
+
+        def unit_gain(h):
+            def drain():
                 for t in range(PACK):
                     nc.scalar.activation(
-                        out=dst[:, t, :], in_=st["turned"][t // 2][:, (t % 2) * PAIR : (t % 2 + 1) * PAIR],
-                        func=COPY, scale=col[:, h, t : t + 1],
+                        out=e[h][:, t, :], in_=e[h][:, t, :], func=COPY, scale=gain_col[:, h, t : t + 1]
+                    )
+
+            return {"drain": drain}
+
+        def unit_kick(q, h):
+            st = {}
+            cols = slice(q * PAIR, (q + 1) * PAIR)
+
+            def matmul():
+                st["sums"] = weights_stationary(a_codes, a_scales, h, x_codes, x_scales, q)
+
+            def add():
+                pairs = d_turned[q, h][:].bitcast(BF16).rearrange("p (u r s) -> p u s r", u=2, s=2)
+                for half in range(2):
+                    nc.vector.tensor_tensor(
+                        out=e[h][:, 2 * half : 2 * half + 2, cols],
+                        in0=st["sums"][half][:].rearrange("p (s r) -> p s r", s=2),
+                        in1=pairs[:, half],
+                        op=ALU.add,
                     )
 
             def drain():
                 st["planes"] = staged("u_planes", [P, PACK, PAIR], BF16, 2)
-                scaled(st["planes"], stride_col)
-
-            def save():
-                eg[q, h] = kept("eg_%d_%d" % (q, h), [P, PACK, PAIR], F32)
-                scaled(eg[q, h], gain_col)
+                for t in range(PACK):
+                    nc.scalar.activation(
+                        out=st["planes"][:, t, :], in_=e[h][:, t, cols], func=COPY,
+                        scale=stride_col[:, h, t : t + 1],
+                    )
 
             def group():
                 st["grouped"] = staged("mode_grouped", [P, PAIR, PACK], BF16, 3)
-                nc.vector.tensor_copy(out=st["grouped"][:], in_=st["planes"][:].rearrange("p t r -> p r t"))
+                interleave("V", st["grouped"], st["planes"])
 
             def quant():
                 quantized("u", u_codes, u_scales, (q, h), st["grouped"][:].rearrange("p r t -> p (r t)"), 6)
 
-            return {"matmul": matmul, "add": add, "turn": turn, "drain": drain, "save": save, "group": group, "quant": quant}
+            return {"matmul": matmul, "add": add, "drain": drain, "group": group, "quant": quant}
 
         def unit_drift(q, g):
             st = {}
@@ -321,27 +347,14 @@ def tile_linear_leapfrog_difference_b9_kernel(
             cols = slice(q * PAIR, (q + 1) * PAIR)
 
             def matmul():
-                st["sums"] = []
-                for half in range(2):
-                    ps = bank("sum")
-                    st["sums"].append(ps)
-                    for s in range(2):
-                        t = 2 * half + s
-                        for g in range(GD):
-                            nc.tensor.matmul_mx(
-                                out=ps[:, s * PAIR : (s + 1) * PAIR],
-                                lhsT=c_codes[h, g][:, t * P : (t + 1) * P].bitcast(FP8X4),
-                                lhsT_scale=c_scales[h, g][:, t * P : (t + 1) * P],
-                                rhs=x1_codes[q, g][:].bitcast(FP8X4), rhs_scale=x1_scales[q, g][:],
-                                start=(g == 0), stop=(g == GD - 1),
-                            )
+                st["sums"] = weights_stationary(c_codes, c_scales, h, x1_codes, x1_scales, q)
 
             def add():
                 st["y"] = staged("y_turned", [P, PACK, PAIR], F32, 3)
                 for t in range(PACK):
                     nc.vector.scalar_tensor_tensor(
                         out=st["y"][:, t, :], in0=st["sums"][t // 2][:, (t % 2) * PAIR : (t % 2 + 1) * PAIR],
-                        scalar=gain_col[:, h, t : t + 1], in1=eg[q, h][:, t, :],
+                        scalar=gain_col[:, h, t : t + 1], in1=e[h][:, t, cols],
                         op0=ALU.mult, op1=ALU.add,
                     )
 
@@ -368,7 +381,7 @@ def tile_linear_leapfrog_difference_b9_kernel(
 
             def group():
                 st["grouped"] = staged("mode_grouped", [P, PAIR, PACK], BF16, 3)
-                copy_on(engine, st["grouped"][:], st["y"][:].rearrange("p t r -> p r t"))
+                interleave(engine, st["grouped"], st["y"])
 
             def quant():
                 y_codes = staged("y_codes", [P, PAIR], U32, 4)
@@ -390,9 +403,37 @@ def tile_linear_leapfrog_difference_b9_kernel(
                 units["D%d%d" % (q, g)] = unit_drift(q, g)
         for q in range(PAIRS):
             for h in range(GF):
+                units["E%d%d" % (q, h)] = unit_d(q, h)
                 units["K%d%d" % (q, h)] = unit_kick(q, h)
                 units["Y%d%d" % (q, h)] = unit_kick2(q, h, "VVVVVV"[q * GF + h])
-        steps = []
+        for h in range(GF):
+            units["G%d" % h] = unit_gain(h)
+        steps = [
+            [units["K00"], units["A10"], units["E01"]],
+            [units["A11"], units["X10"], units["X11"], units["X12"]],
+            [units["A12"], units["E10"], units["E11"]],
+            [],
+            [units["K10"], units["X20"], units["X21"], units["X22"]],
+            [units["K01"], units["E20"], units["E21"]],
+            [units["K11"]],
+            [units["K20"], units["C00"]],
+            [units["D00"]],
+            [units["K21"], units["C01"]],
+            [units["D01"]],
+            [units["D02"], units["C02"]],
+            [units["D10"]],
+            [units["D11"], units["G0"]],
+            [units["D12"], units["C10"]],
+            [units["D20"], units["C11"]],
+            [units["Y00"]],
+            [units["D21"], units["C12"]],
+            [units["D22"]],
+            [units["Y10"], units["G1"]],
+            [units["Y01"]],
+            [units["Y20"]],
+            [units["Y11"]],
+            [units["Y21"]],
+        ]
 
         def run(stage, step):
             if 0 <= step < len(steps):
@@ -400,11 +441,20 @@ def tile_linear_leapfrog_difference_b9_kernel(
                     if stage in unit:
                         unit[stage]()
 
-        for name, stage in [("A00", "drain"), ("A01", "drain"), ("A02", "drain"), ("A00", "group"), ("A01", "group"), ("A00", "quant"), ("A01", "quant"), ("X00", "turn"), ("X01", "turn"), ("X02", "turn"), ("X00", "drain"), ("X01", "drain"), ("X02", "drain"), ("A02", "group"), ("A10", "drain"), ("A02", "quant"), ("X00", "quant"), ("X01", "quant"), ("X02", "quant"), ("X10", "turn"), ("X11", "turn"), ("X12", "turn"), ("K00", "matmul"), ("X10", "drain"), ("X11", "drain"), ("X12", "drain"), ("A11", "drain"), ("A10", "group"), ("X10", "quant"), ("X11", "quant"), ("X12", "quant"), ("K10", "matmul"), ("cols", "group"), ("K00", "add"), ("A10", "quant"), ("K00", "turn"), ("A12", "drain"), ("A11", "group"), ("K10", "add"), ("X20", "turn"), ("X21", "turn"), ("X22", "turn"), ("A11", "quant"), ("K00", "drain"), ("K00", "save"), ("K10", "turn"), ("A12", "group"), ("K00", "group"), ("A12", "quant"), ("K01", "matmul"), ("K11", "matmul"), ("K00", "quant"), ("X20", "drain"), ("X21", "drain"), ("X22", "drain"), ("K10", "drain"), ("K10", "save"), ("C00", "drain"), ("X20", "quant"), ("X21", "quant"), ("X22", "quant"), ("K01", "add"), ("K10", "group"), ("K01", "turn"), ("K20", "matmul"), ("K11", "add"), ("K10", "quant"), ("K01", "drain"), ("K01", "save"), ("K11", "turn"), ("K20", "add"), ("C00", "quant"), ("K21", "matmul"), ("K01", "group"), ("K11", "drain"), ("K11", "save"), ("K01", "quant"), ("K20", "turn"), ("D00", "matmul"), ("K21", "add"), ("K11", "group"), ("K20", "drain"), ("K20", "save"), ("D01", "matmul"), ("D00", "add"), ("K11", "quant"), ("K21", "turn"), ("D02", "matmul"), ("D00", "turn"), ("D01", "add"), ("K20", "group"), ("D00", "drain"), ("K21", "drain"), ("K21", "save"), ("C01", "drain"), ("D10", "matmul"), ("D02", "add"), ("K20", "quant"), ("D01", "turn"), ("D01", "drain"), ("D11", "matmul"), ("D10", "add"), ("D00", "quant"), ("D02", "turn"), ("D02", "drain"), ("C02", "drain"), ("K21", "group"), ("D12", "matmul"), ("D11", "add"), ("D01", "quant"), ("D10", "turn"), ("K21", "quant"), ("C01", "quant"), ("D20", "matmul"), ("D12", "add"), ("D02", "quant"), ("C02", "quant"), ("D10", "drain"), ("D11", "turn"), ("D11", "drain"), ("C10", "drain"), ("Y00", "matmul"), ("D20", "add"), ("D10", "quant"), ("D12", "turn"), ("D12", "drain"), ("D21", "matmul"), ("Y00", "add"), ("D11", "quant"), ("D20", "turn"), ("C10", "quant"), ("D20", "drain"), ("C11", "drain"), ("D22", "matmul"), ("D21", "add"), ("D12", "quant"), ("Y00", "turn"), ("Y00", "group"), ("Y10", "matmul"), ("D22", "add"), ("D20", "quant"), ("D21", "turn"), ("D21", "drain"), ("Y00", "quant"), ("C11", "quant"), ("D22", "turn"), ("D22", "drain"), ("C12", "drain"), ("Y00", "drain"), ("Y10", "add"), ("D21", "quant"), ("D22", "quant"), ("Y20", "matmul"), ("Y10", "group"), ("C12", "quant"), ("Y10", "turn"), ("Y10", "drain"), ("Y01", "matmul"), ("Y20", "add"), ("Y10", "quant"), ("Y20", "turn"), ("Y20", "drain"), ("Y11", "matmul"), ("Y20", "group"), ("Y01", "add"), ("Y20", "quant"), ("Y01", "turn"), ("Y01", "drain"), ("Y21", "matmul"), ("Y01", "group"), ("Y11", "add"), ("Y01", "quant"), ("Y11", "turn"), ("Y11", "drain"), ("Y11", "group"), ("Y21", "add"), ("Y11", "quant"), ("Y21", "turn"), ("Y21", "group"), ("Y21", "drain"), ("Y21", "quant")]:
+        for name, stage in [("A00", "drain"), ("A01", "drain"), ("A00", "group"), ("A02", "drain"), ("A01", "group"), ("A00", "quant"), ("X00", "turn"), ("X01", "turn"), ("X02", "turn"), ("E00", "turn"), ("X00", "drain"), ("X01", "drain"), ("X02", "drain"), ("E00", "drain"), ("A01", "quant"), ("A02", "group"), ("X00", "quant"), ("X01", "quant"), ("A02", "quant"), ("X02", "quant"), ("cols", "group")]:
             units[name][stage]()
+        run("matmul", 0)
+        run("matmul", 1)
+        for s in range(len(steps) + 1):
+            run("group", s - 1)
+            run("add", s)
+            run("turn", s)
+            run("drain", s)
+            run("quant", s - 1)
+            run("matmul", s + 2)
 
         for quad in range(4):
-            nc.sync.dma_start(
+            (nc.sync if quad % 2 else nc.scalar).dma_start(
                 out=out_2[:, 4 * quad : 4 * quad + 4, :].rearrange("g r m -> r g m").bitcast(I32),
                 in_=y_scales[32 * quad : 32 * quad + 4, :, :].bitcast(I32),
             )

@@ -25,6 +25,7 @@ GF = F // KP
 PAIR = 2 * P
 PAIRS = T // PAIR
 BLK = 128
+SPLIT = 1280
 BLOCKS = (D // BLK) * (F // BLK)
 
 
@@ -35,7 +36,7 @@ def tile_linear_leapfrog_difference_b9_kernel(
     with ExitStack() as ctx:
         keep = ctx.enter_context(tc.tile_pool(name="keep", bufs=1))
         work = ctx.enter_context(tc.tile_pool(name="work", bufs=3))
-        psum = ctx.enter_context(tc.psum_pool(name="psum", bufs=4))
+        psum = ctx.enter_context(tc.psum_pool(name="psum", bufs=8))
 
         def kept(name, shape, dtype):
             return keep.tile(shape, dtype, name=name, align_bytes=64)
@@ -44,7 +45,7 @@ def tile_linear_leapfrog_difference_b9_kernel(
             return work.tile(shape, dtype, name=name, tag=name, bufs=bufs, align_bytes=64)
 
         def bank(role):
-            return psum.tile([P, KP], F32, name=role, tag=role)
+            return psum.tile([P, KP], F32, name=role, tag="bank")
 
         def quantize(codes, scales, values):
             nc.vector.quantize_mx(out=codes.bitcast(FP8X4), scales=scales, in_=values)
@@ -52,11 +53,7 @@ def tile_linear_leapfrog_difference_b9_kernel(
         ident = kept("ident", [P, P], F32)
         b_scale = kept("b_scale", [P, GF, D], U8)
 
-        ctx.enter_context(tc.manual_schedule(engines={mybir.EngineType.PE, mybir.EngineType.SP}))
         a_scale_flat = kept("a_scale_flat", [P, 1], F32)
-        nc.gpsimd.memset(a_scale_flat[BLOCKS:P, :], 0.0)
-        make_identity(nc, ident[:])
-        nc.gpsimd.memset(b_scale[:].rearrange("p g n -> p (g n)").bitcast(I32), 0)
         a_raw, c_raw, x_sb, d_sb = {}, {}, {}, {}
 
         def load_a(h, g):
@@ -96,41 +93,14 @@ def tile_linear_leapfrog_difference_b9_kernel(
         stride_raw = kept("stride_raw", [P, GF, PACK], BF16)
         gain_raw = kept("gain_raw", [P, GF, PACK], BF16)
         b_words = kept("b_words", [P, GF, 2 * D], U8)
-        scale_rows = A_scale.rearrange("a (b o) -> (a b) o", o=1)
-        nc.sync.dma_start(out=a_scale_flat[0:64, :], in_=scale_rows[0:64, :])
-        nc.sync.dma_start(out=a_scale_flat[64:BLOCKS, :], in_=scale_rows[64:BLOCKS, :])
-        load_a(0, 0)
-        load_a(0, 1)
-        load_x(0)
-        load_a(0, 2)
-        load_d(0)
-        load_cols()
-        load_x(1)
-        load_a(1, 0)
-        load_d(1)
-        load_a(1, 1)
-        load_x(2)
-        load_a(1, 2)
-        load_d(2)
-        load_c(0)
-        load_b()
-        load_c(1)
-        load_c(2)
-
         a_scale = kept("a_scale", [P, GD, F // BLK], F32)
-        spread = bank("sum")
-        nc.tensor.transpose(spread[:, 0:P], a_scale_flat[:].to_broadcast([P, P]), ident[:])
-        by_row = spread[:, 0:BLOCKS].rearrange("p (g q b) -> p g q b", g=GD, q=4)
-        for quad in range(4):
-            part = slice(32 * quad, 32 * quad + 32)
-            nc.scalar.activation(out=a_scale[part], in_=by_row[part, :, quad, :], func=COPY)
         stride_col = kept("stride_col", [P, GF, PACK], F32)
         gain_col = kept("gain_col", [P, GF, PACK], F32)
 
         a_codes, a_scales, c_codes, c_scales = {}, {}, {}, {}
         x_codes, x_scales, u_codes, u_scales = {}, {}, {}, {}
         x1_codes, x1_scales = {}, {}
-        d_turned = {}
+        d_turned, y_codes = {}, {}
         e = [kept("e_%d" % h, [P, PACK, T], F32) for h in range(GF)]
         y_scales = kept("y_scales", [P, GF, T], U8)
         words_out = out_1.rearrange("g p m t -> g p (m t)").bitcast(I32)
@@ -164,12 +134,14 @@ def tile_linear_leapfrog_difference_b9_kernel(
             st = {}
 
             def widen():
-                st["wide"] = staged("a_wide", [P, PACK, KP], BF16, 2)
-                copy_on(
-                    engine,
-                    st["wide"][:].rearrange("p j f -> p (j f)"),
-                    a_raw[h, g][:].rearrange("p j f -> p (j f)").bitcast(FP8),
-                )
+                st["wide"] = staged("a_wide", [P, PACK, KP], BF16, 3)
+                dst = st["wide"][:].rearrange("p j f -> p (j f)")
+                src = a_raw[h, g][:].rearrange("p j f -> p (j f)").bitcast(FP8)
+                if engine == "H":
+                    copy_on("V", dst[:, :SPLIT], src[:, :SPLIT])
+                    copy_on("S", dst[:, SPLIT:], src[:, SPLIT:])
+                else:
+                    copy_on(engine, dst, src)
 
             def group():
                 st["grouped"] = staged("w_grouped", [P, PACK, P, PACK], BF16, 3)
@@ -220,18 +192,17 @@ def tile_linear_leapfrog_difference_b9_kernel(
 
         def unit_x(q, g):
             st = {}
-            words = x_sb[q][:].bitcast(F32)
             return {
-                "turn": lambda: turn_words(st, lambda i, u: words[:, i, 256 * g + u : 256 * (g + 1) : 2]),
+                "turn": lambda: turn_words(st, lambda i, u: x_sb[q][:].bitcast(F32)[:, i, 256 * g + u : 256 * (g + 1) : 2]),
                 "drain": lambda: drain_words(st),
-                "quant": lambda: quantized("x", x_codes, x_scales, (q, g), st["grouped"][:], 9),
+                "quant": lambda: quantized("pos", x_codes, x_scales, (q, g), st["grouped"][:], 12),
             }
 
         def unit_d(q, h):
             st = {}
-            words = d_sb[q][:].bitcast(F32)
 
             def turn():
+                words = d_sb[q][:].bitcast(F32)
                 st["ps"] = bank("turn")
                 halves = st["ps"][:].rearrange("p (u i r) -> p u i r", i=2, u=2)
                 for u in range(2):
@@ -246,22 +217,24 @@ def tile_linear_leapfrog_difference_b9_kernel(
 
             return {"turn": turn, "drain": drain}
 
-        def weights_stationary(codes, scales, h, moving_codes, moving_scales, q):
-            sums = []
-            for half in range(2):
-                ps = bank("sum")
-                sums.append(ps)
-                for s in range(2):
-                    t = 2 * half + s
-                    for g in range(GD):
-                        nc.tensor.matmul_mx(
-                            out=ps[:, s * PAIR : (s + 1) * PAIR],
-                            lhsT=codes[h, g][:, t * P : (t + 1) * P].bitcast(FP8X4),
-                            lhsT_scale=scales[h, g][:, t * P : (t + 1) * P],
-                            rhs=moving_codes[q, g][:].bitcast(FP8X4), rhs_scale=moving_scales[q, g][:],
-                            start=(g == 0), stop=(g == GD - 1),
-                        )
-            return sums
+        def weights_stationary(codes, scales, h, moving_codes, moving_scales, q, rows):
+            width = rows.stop - rows.start
+            sums, banks = [], []
+            for t in range(PACK):
+                s = t % (KP // width)
+                if s == 0:
+                    ps = bank("sum")
+                    banks.append(ps)
+                sums.append(ps[:, s * width : (s + 1) * width])
+                for g in range(GD):
+                    nc.tensor.matmul_mx(
+                        out=sums[t],
+                        lhsT=codes[h, g][:, t * P : (t + 1) * P].bitcast(FP8X4),
+                        lhsT_scale=scales[h, g][:, t * P : (t + 1) * P],
+                        rhs=moving_codes[q, g][:, rows].bitcast(FP8X4), rhs_scale=moving_scales[q, g][:, rows],
+                        start=(g == 0), stop=(g == GD - 1),
+                    )
+            return sums, banks
 
         def unit_gain(h):
             def drain():
@@ -277,7 +250,7 @@ def tile_linear_leapfrog_difference_b9_kernel(
             cols = slice(q * PAIR, (q + 1) * PAIR)
 
             def matmul():
-                st["sums"] = weights_stationary(a_codes, a_scales, h, x_codes, x_scales, q)
+                st["sums"] = weights_stationary(a_codes, a_scales, h, x_codes, x_scales, q, slice(0, PAIR))[1]
 
             def add():
                 pairs = d_turned[q, h][:].bitcast(BF16).rearrange("p (u r s) -> p u s r", u=2, s=2)
@@ -339,28 +312,30 @@ def tile_linear_leapfrog_difference_b9_kernel(
                 "add": add,
                 "turn": lambda: turn_words(st, lambda i, u: st["x1"][:].bitcast(F32)[:, i, u * P : (u + 1) * P]),
                 "drain": lambda: drain_words(st),
-                "quant": lambda: quantized("x1", x1_codes, x1_scales, (q, g), st["grouped"][:], 9),
+                "quant": lambda: quantized("pos", x1_codes, x1_scales, (q, g), st["grouped"][:], 12),
             }
 
-        def unit_kick2(q, h, engine):
+        def unit_kick2(q, h, engine, first=0, tiles=2):
             st = {}
-            cols = slice(q * PAIR, (q + 1) * PAIR)
+            width = tiles * P
+            rows = slice(first * P, first * P + width)
+            cols = slice(q * PAIR + rows.start, q * PAIR + rows.stop)
 
             def matmul():
-                st["sums"] = weights_stationary(c_codes, c_scales, h, x1_codes, x1_scales, q)
+                st["sums"] = weights_stationary(c_codes, c_scales, h, x1_codes, x1_scales, q, rows)[0]
 
             def add():
-                st["y"] = staged("y_turned", [P, PACK, PAIR], F32, 3)
+                st["y"] = staged("y_turned", [P, PACK, width], F32, 3)
                 for t in range(PACK):
                     nc.vector.scalar_tensor_tensor(
-                        out=st["y"][:, t, :], in0=st["sums"][t // 2][:, (t % 2) * PAIR : (t % 2 + 1) * PAIR],
+                        out=st["y"][:, t, :], in0=st["sums"][t],
                         scalar=gain_col[:, h, t : t + 1], in1=e[h][:, t, cols],
                         op0=ALU.mult, op1=ALU.add,
                     )
 
             def turn():
                 st["turned"] = []
-                for i in range(2):
+                for i in range(tiles):
                     ps = bank("turn")
                     st["turned"].append(ps)
                     for t in range(PACK):
@@ -371,22 +346,26 @@ def tile_linear_leapfrog_difference_b9_kernel(
             def drain():
                 if engine == "S":
                     group()
-                for i in range(2):
-                    y = staged("y", [P, P, PACK], F32, 4)
-                    nc.scalar.copy(out=y[:], in_=st["turned"][i][:].rearrange("r (t m) -> r m t", t=PACK))
-                    rows = slice(q * PAIR + i * P, q * PAIR + (i + 1) * P)
-                    nc.sync.dma_start(
-                        out=out_0[rows, h * KP : (h + 1) * KP], in_=y[:].rearrange("r m t -> r (m t)")
-                    )
+                y = staged("y", [P, tiles, P, PACK], F32, 3)
+                for i in range(tiles):
+                    nc.scalar.copy(out=y[:, i], in_=st["turned"][i][:].rearrange("r (t m) -> r m t", t=PACK))
+                nc.sync.dma_start(
+                    out=out_0[cols, h * KP : (h + 1) * KP].rearrange("(i r) f -> r i f", r=P),
+                    in_=y[:].rearrange("r i m t -> r i (m t)"),
+                )
 
             def group():
-                st["grouped"] = staged("mode_grouped", [P, PAIR, PACK], BF16, 3)
+                st["grouped"] = staged("mode_grouped", [P, width, PACK], BF16, 3)
                 interleave(engine, st["grouped"], st["y"])
 
             def quant():
-                y_codes = staged("y_codes", [P, PAIR], U32, 4)
-                quantize(y_codes[:], y_scales[:, h, cols], st["grouped"][:].rearrange("p r t -> p (r t)"))
-                nc.sync.dma_start(out=words_out[h, :, cols], in_=y_codes[:].bitcast(I32))
+                if first == 0:
+                    y_codes[q, h] = staged("y_codes", [P, PAIR], U32, 3)
+                quantize(y_codes[q, h][:, rows], y_scales[:, h, cols], st["grouped"][:].rearrange("p r t -> p (r t)"))
+                if rows.stop == PAIR:
+                    nc.sync.dma_start(
+                        out=words_out[h, :, q * PAIR : (q + 1) * PAIR], in_=y_codes[q, h][:].bitcast(I32)
+                    )
 
             stages = {"matmul": matmul, "add": add, "turn": turn, "drain": drain, "quant": quant}
             if engine == "V":
@@ -396,8 +375,8 @@ def tile_linear_leapfrog_difference_b9_kernel(
         units = {"cols": unit_cols()}
         for g in range(GD):
             for h in range(GF):
-                units["A%d%d" % (h, g)] = unit_a(h, g, "VSSVSS"[h * GD + g])
-                units["C%d%d" % (h, g)] = unit_c(h, g, "SSSSSS"[h * GD + g])
+                units["A%d%d" % (h, g)] = unit_a(h, g, "HSSVSS"[h * GD + g])
+                units["C%d%d" % (h, g)] = unit_c(h, g, "VSSSSS"[h * GD + g])
             for q in range(PAIRS):
                 units["X%d%d" % (q, g)] = unit_x(q, g)
                 units["D%d%d" % (q, g)] = unit_drift(q, g)
@@ -405,34 +384,33 @@ def tile_linear_leapfrog_difference_b9_kernel(
             for h in range(GF):
                 units["E%d%d" % (q, h)] = unit_d(q, h)
                 units["K%d%d" % (q, h)] = unit_kick(q, h)
-                units["Y%d%d" % (q, h)] = unit_kick2(q, h, "VVVVVV"[q * GF + h])
+                units["Y%d%d" % (q, h)] = unit_kick2(q, h, "VVSVSV"[q * GF + h])
         for h in range(GF):
             units["G%d" % h] = unit_gain(h)
+        units["Za"] = unit_kick2(2, 1, "V", 0, 1)
+        units["Zb"] = unit_kick2(2, 1, "V", 1, 1)
         steps = [
             [units["K00"], units["A10"], units["E01"]],
             [units["A11"], units["X10"], units["X11"], units["X12"]],
             [units["A12"], units["E10"], units["E11"]],
-            [],
-            [units["K10"], units["X20"], units["X21"], units["X22"]],
-            [units["K01"], units["E20"], units["E21"]],
+            [units["X20"], units["X21"], units["X22"]],
+            [units["K10"], units["E20"], units["E21"]],
+            [units["K01"]],
             [units["K11"]],
             [units["K20"], units["C00"]],
-            [units["D00"]],
             [units["K21"], units["C01"]],
-            [units["D01"]],
-            [units["D02"], units["C02"]],
-            [units["D10"]],
-            [units["D11"], units["G0"]],
-            [units["D12"], units["C10"]],
-            [units["D20"], units["C11"]],
-            [units["Y00"]],
-            [units["D21"], units["C12"]],
-            [units["D22"]],
-            [units["Y10"], units["G1"]],
+            [units["D00"], units["D01"], units["C02"]],
+            [units["D02"], units["G0"]],
+            [units["D10"], units["D11"], units["C10"]],
+            [units["D12"], units["D20"], units["C11"]],
+            [units["Y00"], units["C12"]],
+            [units["D21"], units["D22"], units["G1"]],
+            [units["Y10"]],
             [units["Y01"]],
             [units["Y20"]],
             [units["Y11"]],
-            [units["Y21"]],
+            [units["Za"]],
+            [units["Zb"]],
         ]
 
         def run(stage, step):
@@ -441,17 +419,50 @@ def tile_linear_leapfrog_difference_b9_kernel(
                     if stage in unit:
                         unit[stage]()
 
-        for name, stage in [("A00", "drain"), ("A01", "drain"), ("A00", "group"), ("A02", "drain"), ("A01", "group"), ("A00", "quant"), ("X00", "turn"), ("X01", "turn"), ("X02", "turn"), ("E00", "turn"), ("X00", "drain"), ("X01", "drain"), ("X02", "drain"), ("E00", "drain"), ("A01", "quant"), ("A02", "group"), ("X00", "quant"), ("X01", "quant"), ("A02", "quant"), ("X02", "quant"), ("cols", "group")]:
-            units[name][stage]()
-        run("matmul", 0)
-        run("matmul", 1)
-        for s in range(len(steps) + 1):
-            run("group", s - 1)
-            run("add", s)
-            run("turn", s)
-            run("drain", s)
-            run("quant", s - 1)
-            run("matmul", s + 2)
+        with tc.manual_schedule():
+            nc.gpsimd.memset(a_scale_flat[BLOCKS:P, :], 0.0)
+            make_identity(nc, ident[:])
+            nc.gpsimd.memset(b_scale[:].rearrange("p g n -> p (g n)").bitcast(I32), 0)
+            load_a(0, 0)
+            scale_rows = A_scale.rearrange("a (b o) -> (a b) o", o=1)
+            nc.sync.dma_start(out=a_scale_flat[0:64, :], in_=scale_rows[0:64, :])
+            nc.sync.dma_start(out=a_scale_flat[64:BLOCKS, :], in_=scale_rows[64:BLOCKS, :])
+            load_a(0, 1)
+            load_x(0)
+            load_a(0, 2)
+            load_a(1, 0)
+            load_d(0)
+            load_cols()
+            load_a(1, 1)
+            load_a(1, 2)
+            load_x(1)
+            load_d(1)
+            load_x(2)
+            load_d(2)
+            load_c(0)
+            load_b()
+            load_c(1)
+            load_c(2)
+
+            spread = bank("sum")
+            nc.tensor.transpose(spread[:, 0:P], a_scale_flat[:].to_broadcast([P, P]), ident[:])
+            by_row = spread[:, 0:BLOCKS].rearrange("p (g q b) -> p g q b", g=GD, q=4)
+            for quad in range(4):
+                part = slice(32 * quad, 32 * quad + 32)
+                nc.scalar.activation(out=a_scale[part], in_=by_row[part, :, quad, :], func=COPY)
+            for name, stage in [("A00", "drain"), ("A01", "drain"), ("A00", "group"), ("A02", "drain"), ("A01", "group"), ("A00", "quant"), ("X00", "turn"), ("X01", "turn"), ("X02", "turn"), ("E00", "turn"), ("X00", "drain"), ("X01", "drain"), ("X02", "drain"), ("E00", "drain"), ("A01", "quant"), ("A02", "group"), ("X00", "quant"), ("X01", "quant"), ("A02", "quant"), ("X02", "quant"), ("cols", "group")]:
+                units[name][stage]()
+
+        with tc.manual_schedule(engines={mybir.EngineType.PE}):
+            run("matmul", 0)
+            run("matmul", 1)
+            for s in range(len(steps) + 1):
+                run("group", s - 1)
+                run("add", s)
+                run("turn", s)
+                run("drain", s)
+                run("quant", s - 1)
+                run("matmul", s + 2)
 
         for quad in range(4):
             (nc.sync if quad % 2 else nc.scalar).dma_start(

@@ -16,6 +16,7 @@ FP8X4 = mybir.dt.float8_e4m3fn_x4
 FP4X4 = mybir.dt.float4_e2m1fn_x4
 ALU = mybir.AluOpType
 COPY = mybir.ActivationFunctionType.Copy
+VECTOR, SCALAR = "vector", "scalar"
 
 P = 128
 PACK = 4
@@ -25,8 +26,10 @@ GF = F // KP
 PAIR = 2 * P
 PAIRS = T // PAIR
 BLK = 128
-SPLIT = 1280
 BLOCKS = (D // BLK) * (F // BLK)
+QUADS = 4
+SPLIT = 1280
+LEAD = 3
 
 
 def tile_linear_leapfrog_difference_b9_kernel(
@@ -47,19 +50,34 @@ def tile_linear_leapfrog_difference_b9_kernel(
         def bank(role):
             return psum.tile([P, KP], F32, name=role, tag="bank")
 
-        def quantize(codes, scales, values):
-            nc.vector.quantize_mx(out=codes.bitcast(FP8X4), scales=scales, in_=values)
-
         ident = kept("ident", [P, P], F32)
-        b_scale = kept("b_scale", [P, GF, D], U8)
-
         a_scale_flat = kept("a_scale_flat", [P, 1], F32)
+        a_scale = kept("a_scale", [P, GD, F // BLK], F32)
+        b_words = kept("b_words", [P, GF, 2 * D], U8)
+        b_scale = kept("b_scale", [P, GF, D], U8)
+        stride_raw = kept("stride_raw", [P, GF, PACK], BF16)
+        gain_raw = kept("gain_raw", [P, GF, PACK], BF16)
+        stride_col = kept("stride_col", [P, GF, PACK], F32)
+        gain_col = kept("gain_col", [P, GF, PACK], F32)
+        e = [kept("e_%d" % h, [P, PACK, T], F32) for h in range(GF)]
+        y_scales = kept("y_scales", [P, GF, T], U8)
+        words_out = out_1.rearrange("g p m t -> g p (m t)").bitcast(I32)
+
         a_raw, c_raw, x_sb, d_sb = {}, {}, {}, {}
+        a_codes, a_scales, c_codes, c_scales = {}, {}, {}, {}
+        x_codes, x_scales, x1_codes, x1_scales = {}, {}, {}, {}
+        u_codes, u_scales, y_codes, d_turned = {}, {}, {}, {}
+
 
         def load_a(h, g):
             a_raw[h, g] = kept("a_bytes_%d_%d" % (h, g), [P, PACK, KP], U8)
             rows = A_bytes[g * KP : (g + 1) * KP, h * KP : (h + 1) * KP]
             nc.sync.dma_start(out=a_raw[h, g][:], in_=rows.rearrange("(p j) f -> p j f", j=PACK))
+
+        def load_a_scale():
+            flat = A_scale.rearrange("a (b o) -> (a b) o", o=1)
+            nc.sync.dma_start(out=a_scale_flat[0:64, :], in_=flat[0:64, :])
+            nc.sync.dma_start(out=a_scale_flat[64:BLOCKS, :], in_=flat[64:BLOCKS, :])
 
         def load_c(g):
             c_raw[g] = kept("c_raw_%d" % g, [P, PACK, F], BF16)
@@ -76,12 +94,12 @@ def tile_linear_leapfrog_difference_b9_kernel(
             rows = d[q * PAIR : (q + 1) * PAIR, :]
             nc.sync.dma_start(out=d_sb[q][:], in_=rows.rearrange("(i p) f -> p i f", p=P))
 
-        def load_cols():
+        def load_stride_gain():
             nc.sync.dma_start(out=stride_raw[:], in_=stride.rearrange("o (g p t) -> p (o g) t", p=P, t=PACK))
             nc.sync.dma_start(out=gain_raw[:], in_=gain.rearrange("o (g p t) -> p (o g) t", p=P, t=PACK))
 
         def load_b():
-            for quad in range(4):
+            for quad in range(QUADS):
                 nc.sync.dma_start(
                     out=b_scale[32 * quad : 32 * quad + 4, :, :].bitcast(I32),
                     in_=B_scales[:, 4 * quad : 4 * quad + 4, :].rearrange("g r n -> r g n").bitcast(I32),
@@ -90,58 +108,75 @@ def tile_linear_leapfrog_difference_b9_kernel(
                 out=b_words[:].bitcast(I32), in_=B_words.rearrange("g p n -> p g n").bitcast(I32)
             )
 
-        stride_raw = kept("stride_raw", [P, GF, PACK], BF16)
-        gain_raw = kept("gain_raw", [P, GF, PACK], BF16)
-        b_words = kept("b_words", [P, GF, 2 * D], U8)
-        a_scale = kept("a_scale", [P, GD, F // BLK], F32)
-        stride_col = kept("stride_col", [P, GF, PACK], F32)
-        gain_col = kept("gain_col", [P, GF, PACK], F32)
-
-        a_codes, a_scales, c_codes, c_scales = {}, {}, {}, {}
-        x_codes, x_scales, u_codes, u_scales = {}, {}, {}, {}
-        x1_codes, x1_scales = {}, {}
-        d_turned, y_codes = {}, {}
-        e = [kept("e_%d" % h, [P, PACK, T], F32) for h in range(GF)]
-        y_scales = kept("y_scales", [P, GF, T], U8)
-        words_out = out_1.rearrange("g p m t -> g p (m t)").bitcast(I32)
 
         def copy_on(engine, out, in_):
-            if engine == "V":
+            if engine == VECTOR:
                 nc.vector.tensor_copy(out=out, in_=in_)
             else:
                 nc.scalar.copy(out=out, in_=in_)
 
-        def interleave(engine, grouped, planes):
+        def interleave(engine, grouped, slices):
             copy_on(
                 engine,
                 grouped[:].rearrange("p (c i) t -> p c t i", i=PACK),
-                planes[:].rearrange("p t (c i) -> p c t i", i=PACK),
+                slices[:].rearrange("p t (c i) -> p c t i", i=PACK),
             )
 
-        def quantized(name, codes, scales, key, grouped, bufs):
+        def quantize(codes, scales, grouped):
+            nc.vector.quantize_mx(out=codes.bitcast(FP8X4), scales=scales, in_=grouped)
+
+        def quantize_into(name, codes, scales, key, grouped, bufs):
             width = grouped.shape[1] // PACK
             codes[key] = staged(name + "_codes", [P, width], U32, bufs)
             scales[key] = staged(name + "_scales", [P, width], U8, bufs)
             quantize(codes[key][:], scales[key][:], grouped)
 
-        def unit_cols():
-            def group():
-                nc.vector.tensor_copy(out=stride_col[:], in_=stride_raw[:])
-                nc.vector.tensor_copy(out=gain_col[:], in_=gain_raw[:])
-            return {"group": group}
+        def turn_words(st, words):
+            st["ps"] = bank("turn")
+            parts = st["ps"][:].rearrange("p (i u r) -> p i u r", i=2, u=2)
+            for i in range(2):
+                for u in range(2):
+                    nc.tensor.transpose(parts[:, i, u, :], words(i, u), ident[:])
 
-        def unit_a(h, g, engine):
+        def drain_words(st):
+            st["grouped"] = staged("pos_grouped", [P, PAIR * PACK], BF16, 4)
+            nc.scalar.copy(
+                out=st["grouped"][:].bitcast(F32).rearrange("p (i r u) -> p i r u", i=2, u=2),
+                in_=st["ps"][:].rearrange("p (i u r) -> p i r u", i=2, u=2),
+            )
+
+        def kick_matmuls(w_codes, w_scales, h, pos_codes, pos_scales, q, rows):
+            width = rows.stop - rows.start
+            sums, banks = [], []
+            for t in range(PACK):
+                place = t % (KP // width)
+                if place == 0:
+                    banks.append(bank("sum"))
+                sums.append(banks[-1][:, place * width : (place + 1) * width])
+                for g in range(GD):
+                    nc.tensor.matmul_mx(
+                        out=sums[t],
+                        lhsT=w_codes[h, g][:, t * P : (t + 1) * P].bitcast(FP8X4),
+                        lhsT_scale=w_scales[h, g][:, t * P : (t + 1) * P],
+                        rhs=pos_codes[q, g][:, rows].bitcast(FP8X4),
+                        rhs_scale=pos_scales[q, g][:, rows],
+                        start=(g == 0),
+                        stop=(g == GD - 1),
+                    )
+            return sums, banks
+
+
+        def unit_a(h, g, vector_cols):
             st = {}
 
             def widen():
                 st["wide"] = staged("a_wide", [P, PACK, KP], BF16, 3)
                 dst = st["wide"][:].rearrange("p j f -> p (j f)")
                 src = a_raw[h, g][:].rearrange("p j f -> p (j f)").bitcast(FP8)
-                if engine == "H":
-                    copy_on("V", dst[:, :SPLIT], src[:, :SPLIT])
-                    copy_on("S", dst[:, SPLIT:], src[:, SPLIT:])
-                else:
-                    copy_on(engine, dst, src)
+                if vector_cols > 0:
+                    nc.vector.tensor_copy(out=dst[:, :vector_cols], in_=src[:, :vector_cols])
+                if vector_cols < PACK * KP:
+                    nc.scalar.copy(out=dst[:, vector_cols:], in_=src[:, vector_cols:])
 
             def group():
                 st["grouped"] = staged("w_grouped", [P, PACK, P, PACK], BF16, 3)
@@ -156,7 +191,8 @@ def tile_linear_leapfrog_difference_b9_kernel(
                     )
 
             def quant():
-                quantized("a", a_codes, a_scales, (h, g), st["grouped"][:].rearrange("p t m j -> p (t m j)"), 6)
+                grouped = st["grouped"][:].rearrange("p t m j -> p (t m j)")
+                quantize_into("a", a_codes, a_scales, (h, g), grouped, GF * GD)
 
             return {"drain": widen, "group": group, "quant": quant}
 
@@ -172,30 +208,21 @@ def tile_linear_leapfrog_difference_b9_kernel(
                 )
 
             def quant():
-                quantized("c", c_codes, c_scales, (h, g), st["grouped"][:].rearrange("p t m j -> p (t m j)"), 6)
+                grouped = st["grouped"][:].rearrange("p t m j -> p (t m j)")
+                quantize_into("c", c_codes, c_scales, (h, g), grouped, GF * GD)
 
-            return {"group" if engine == "V" else "drain": group, "quant": quant}
-
-        def turn_words(st, source):
-            st["ps"] = bank("turn")
-            halves = st["ps"][:].rearrange("p (i u r) -> p i u r", i=2, u=2)
-            for i in range(2):
-                for u in range(2):
-                    nc.tensor.transpose(halves[:, i, u, :], source(i, u), ident[:])
-
-        def drain_words(st):
-            st["grouped"] = staged("pos_grouped", [P, PAIR * PACK], BF16, 4)
-            nc.scalar.copy(
-                out=st["grouped"][:].bitcast(F32).rearrange("p (i r u) -> p i r u", i=2, u=2),
-                in_=st["ps"][:].rearrange("p (i u r) -> p i r u", i=2, u=2),
-            )
+            return {"group" if engine == VECTOR else "drain": group, "quant": quant}
 
         def unit_x(q, g):
             st = {}
+
+            def words(i, u):
+                return x_sb[q][:].bitcast(F32)[:, i, 256 * g + u : 256 * (g + 1) : 2]
+
             return {
-                "turn": lambda: turn_words(st, lambda i, u: x_sb[q][:].bitcast(F32)[:, i, 256 * g + u : 256 * (g + 1) : 2]),
+                "turn": lambda: turn_words(st, words),
                 "drain": lambda: drain_words(st),
-                "quant": lambda: quantized("pos", x_codes, x_scales, (q, g), st["grouped"][:], 12),
+                "quant": lambda: quantize_into("pos", x_codes, x_scales, (q, g), st["grouped"][:], 12),
             }
 
         def unit_d(q, h):
@@ -204,11 +231,11 @@ def tile_linear_leapfrog_difference_b9_kernel(
             def turn():
                 words = d_sb[q][:].bitcast(F32)
                 st["ps"] = bank("turn")
-                halves = st["ps"][:].rearrange("p (u i r) -> p u i r", i=2, u=2)
+                parts = st["ps"][:].rearrange("p (u i r) -> p u i r", i=2, u=2)
                 for u in range(2):
                     for i in range(2):
                         nc.tensor.transpose(
-                            halves[:, u, i, :], words[:, i, 256 * h + u : 256 * (h + 1) : 2], ident[:]
+                            parts[:, u, i, :], words[:, i, 256 * h + u : 256 * (h + 1) : 2], ident[:]
                         )
 
             def drain():
@@ -217,24 +244,80 @@ def tile_linear_leapfrog_difference_b9_kernel(
 
             return {"turn": turn, "drain": drain}
 
-        def weights_stationary(codes, scales, h, moving_codes, moving_scales, q, rows):
-            width = rows.stop - rows.start
-            sums, banks = [], []
-            for t in range(PACK):
-                s = t % (KP // width)
-                if s == 0:
-                    ps = bank("sum")
-                    banks.append(ps)
-                sums.append(ps[:, s * width : (s + 1) * width])
-                for g in range(GD):
-                    nc.tensor.matmul_mx(
-                        out=sums[t],
-                        lhsT=codes[h, g][:, t * P : (t + 1) * P].bitcast(FP8X4),
-                        lhsT_scale=scales[h, g][:, t * P : (t + 1) * P],
-                        rhs=moving_codes[q, g][:, rows].bitcast(FP8X4), rhs_scale=moving_scales[q, g][:, rows],
-                        start=(g == 0), stop=(g == GD - 1),
+        def unit_first_kick(q, h):
+            st = {}
+            cols = slice(q * PAIR, (q + 1) * PAIR)
+
+            def matmul():
+                st["banks"] = kick_matmuls(a_codes, a_scales, h, x_codes, x_scales, q, slice(0, PAIR))[1]
+
+            def add():
+                halves = d_turned[q, h][:].bitcast(BF16).rearrange("p (u r s) -> p u s r", u=2, s=2)
+                for u in range(2):
+                    nc.vector.tensor_tensor(
+                        out=e[h][:, 2 * u : 2 * u + 2, cols],
+                        in0=st["banks"][u][:].rearrange("p (s r) -> p s r", s=2),
+                        in1=halves[:, u],
+                        op=ALU.add,
                     )
-            return sums, banks
+
+            def drain():
+                st["slices"] = staged("u_slices", [P, PACK, PAIR], BF16, 2)
+                for t in range(PACK):
+                    nc.scalar.activation(
+                        out=st["slices"][:, t, :], in_=e[h][:, t, cols], func=COPY,
+                        scale=stride_col[:, h, t : t + 1],
+                    )
+
+            def group():
+                st["grouped"] = staged("mode_grouped", [P, PAIR, PACK], BF16, 3)
+                interleave(VECTOR, st["grouped"], st["slices"])
+
+            def quant():
+                grouped = st["grouped"][:].rearrange("p r t -> p (r t)")
+                quantize_into("u", u_codes, u_scales, (q, h), grouped, PAIRS * GF)
+
+            return {"matmul": matmul, "add": add, "drain": drain, "group": group, "quant": quant}
+
+        def unit_drift(q, g):
+            st = {}
+
+            def matmul():
+                st["banks"] = []
+                for i in range(2):
+                    st["banks"].append(bank("sum"))
+                    cols = slice(i * P, (i + 1) * P)
+                    for h in range(GF):
+                        nc.tensor.matmul_mx(
+                            out=st["banks"][i][:],
+                            lhsT=u_codes[q, h][:, cols].bitcast(FP8X4),
+                            lhsT_scale=u_scales[q, h][:, cols],
+                            rhs=b_words[:, h, 2 * KP * g : 2 * KP * (g + 1)].bitcast(FP4X4),
+                            rhs_scale=b_scale[:, h, KP * g : KP * (g + 1)],
+                            start=(h == 0),
+                            stop=(h == GF - 1),
+                        )
+
+            def add():
+                st["x1"] = staged("x1", [P, 2, KP], BF16, 2)
+                for i in range(2):
+                    nc.vector.tensor_tensor(
+                        out=st["x1"][:, i, :].rearrange("p (u m s) -> p u m s", u=2, s=2),
+                        in0=st["banks"][i][:].rearrange("p (m u s) -> p u m s", u=2, s=2),
+                        in1=x_sb[q][:, i, g * KP : (g + 1) * KP].rearrange("p (m u s) -> p u m s", u=2, s=2),
+                        op=ALU.add,
+                    )
+
+            def words(i, u):
+                return st["x1"][:].bitcast(F32)[:, i, u * P : (u + 1) * P]
+
+            return {
+                "matmul": matmul,
+                "add": add,
+                "turn": lambda: turn_words(st, words),
+                "drain": lambda: drain_words(st),
+                "quant": lambda: quantize_into("pos", x1_codes, x1_scales, (q, g), st["grouped"][:], 12),
+            }
 
         def unit_gain(h):
             def drain():
@@ -245,84 +328,14 @@ def tile_linear_leapfrog_difference_b9_kernel(
 
             return {"drain": drain}
 
-        def unit_kick(q, h):
-            st = {}
-            cols = slice(q * PAIR, (q + 1) * PAIR)
-
-            def matmul():
-                st["sums"] = weights_stationary(a_codes, a_scales, h, x_codes, x_scales, q, slice(0, PAIR))[1]
-
-            def add():
-                pairs = d_turned[q, h][:].bitcast(BF16).rearrange("p (u r s) -> p u s r", u=2, s=2)
-                for half in range(2):
-                    nc.vector.tensor_tensor(
-                        out=e[h][:, 2 * half : 2 * half + 2, cols],
-                        in0=st["sums"][half][:].rearrange("p (s r) -> p s r", s=2),
-                        in1=pairs[:, half],
-                        op=ALU.add,
-                    )
-
-            def drain():
-                st["planes"] = staged("u_planes", [P, PACK, PAIR], BF16, 2)
-                for t in range(PACK):
-                    nc.scalar.activation(
-                        out=st["planes"][:, t, :], in_=e[h][:, t, cols], func=COPY,
-                        scale=stride_col[:, h, t : t + 1],
-                    )
-
-            def group():
-                st["grouped"] = staged("mode_grouped", [P, PAIR, PACK], BF16, 3)
-                interleave("V", st["grouped"], st["planes"])
-
-            def quant():
-                quantized("u", u_codes, u_scales, (q, h), st["grouped"][:].rearrange("p r t -> p (r t)"), 6)
-
-            return {"matmul": matmul, "add": add, "drain": drain, "group": group, "quant": quant}
-
-        def unit_drift(q, g):
-            st = {}
-
-            def matmul():
-                st["sums"] = []
-                for i in range(2):
-                    ps = bank("sum")
-                    st["sums"].append(ps)
-                    cols = slice(i * P, (i + 1) * P)
-                    for h in range(GF):
-                        nc.tensor.matmul_mx(
-                            out=ps[:],
-                            lhsT=u_codes[q, h][:, cols].bitcast(FP8X4), lhsT_scale=u_scales[q, h][:, cols],
-                            rhs=b_words[:, h, 2 * KP * g : 2 * KP * (g + 1)].bitcast(FP4X4),
-                            rhs_scale=b_scale[:, h, KP * g : KP * (g + 1)],
-                            start=(h == 0), stop=(h == GF - 1),
-                        )
-
-            def add():
-                st["x1"] = staged("x1", [P, 2, KP], BF16, 2)
-                for i in range(2):
-                    nc.vector.tensor_tensor(
-                        out=st["x1"][:, i, :].rearrange("p (u m e) -> p u m e", u=2, e=2),
-                        in0=st["sums"][i][:].rearrange("p (m u e) -> p u m e", u=2, e=2),
-                        in1=x_sb[q][:, i, g * KP : (g + 1) * KP].rearrange("p (m u e) -> p u m e", u=2, e=2),
-                        op=ALU.add,
-                    )
-
-            return {
-                "matmul": matmul,
-                "add": add,
-                "turn": lambda: turn_words(st, lambda i, u: st["x1"][:].bitcast(F32)[:, i, u * P : (u + 1) * P]),
-                "drain": lambda: drain_words(st),
-                "quant": lambda: quantized("pos", x1_codes, x1_scales, (q, g), st["grouped"][:], 12),
-            }
-
-        def unit_kick2(q, h, engine, first=0, tiles=2):
+        def unit_second_kick(q, h, engine, first, tiles):
             st = {}
             width = tiles * P
             rows = slice(first * P, first * P + width)
             cols = slice(q * PAIR + rows.start, q * PAIR + rows.stop)
 
             def matmul():
-                st["sums"] = weights_stationary(c_codes, c_scales, h, x1_codes, x1_scales, q, rows)[0]
+                st["sums"] = kick_matmuls(c_codes, c_scales, h, x1_codes, x1_scales, q, rows)[0]
 
             def add():
                 st["y"] = staged("y_turned", [P, PACK, width], F32, 3)
@@ -334,88 +347,77 @@ def tile_linear_leapfrog_difference_b9_kernel(
                     )
 
             def turn():
-                st["turned"] = []
+                st["banks"] = []
                 for i in range(tiles):
-                    ps = bank("turn")
-                    st["turned"].append(ps)
+                    st["banks"].append(bank("turn"))
                     for t in range(PACK):
                         nc.tensor.transpose(
-                            ps[:, t * P : (t + 1) * P], st["y"][:, t, i * P : (i + 1) * P], ident[:]
+                            st["banks"][i][:, t * P : (t + 1) * P], st["y"][:, t, i * P : (i + 1) * P], ident[:]
                         )
-
-            def drain():
-                if engine == "S":
-                    group()
-                y = staged("y", [P, tiles, P, PACK], F32, 3)
-                for i in range(tiles):
-                    nc.scalar.copy(out=y[:, i], in_=st["turned"][i][:].rearrange("r (t m) -> r m t", t=PACK))
-                nc.sync.dma_start(
-                    out=out_0[cols, h * KP : (h + 1) * KP].rearrange("(i r) f -> r i f", r=P),
-                    in_=y[:].rearrange("r i m t -> r i (m t)"),
-                )
 
             def group():
                 st["grouped"] = staged("mode_grouped", [P, width, PACK], BF16, 3)
                 interleave(engine, st["grouped"], st["y"])
 
+            def drain():
+                if engine == SCALAR:
+                    group()
+                y_rows = staged("y_rows", [P, tiles, P, PACK], F32, 3)
+                for i in range(tiles):
+                    nc.scalar.copy(out=y_rows[:, i], in_=st["banks"][i][:].rearrange("r (t m) -> r m t", t=PACK))
+                nc.sync.dma_start(
+                    out=out_0[cols, h * KP : (h + 1) * KP].rearrange("(i r) f -> r i f", r=P),
+                    in_=y_rows[:].rearrange("r i m t -> r i (m t)"),
+                )
+
             def quant():
                 if first == 0:
                     y_codes[q, h] = staged("y_codes", [P, PAIR], U32, 3)
-                quantize(y_codes[q, h][:, rows], y_scales[:, h, cols], st["grouped"][:].rearrange("p r t -> p (r t)"))
+                grouped = st["grouped"][:].rearrange("p r t -> p (r t)")
+                quantize(y_codes[q, h][:, rows], y_scales[:, h, cols], grouped)
                 if rows.stop == PAIR:
                     nc.sync.dma_start(
                         out=words_out[h, :, q * PAIR : (q + 1) * PAIR], in_=y_codes[q, h][:].bitcast(I32)
                     )
 
             stages = {"matmul": matmul, "add": add, "turn": turn, "drain": drain, "quant": quant}
-            if engine == "V":
+            if engine == VECTOR:
                 stages["group"] = group
             return stages
 
-        units = {"cols": unit_cols()}
-        for g in range(GD):
-            for h in range(GF):
-                units["A%d%d" % (h, g)] = unit_a(h, g, "HSSVSS"[h * GD + g])
-                units["C%d%d" % (h, g)] = unit_c(h, g, "VSSSSS"[h * GD + g])
-            for q in range(PAIRS):
-                units["X%d%d" % (q, g)] = unit_x(q, g)
-                units["D%d%d" % (q, g)] = unit_drift(q, g)
-        for q in range(PAIRS):
-            for h in range(GF):
-                units["E%d%d" % (q, h)] = unit_d(q, h)
-                units["K%d%d" % (q, h)] = unit_kick(q, h)
-                units["Y%d%d" % (q, h)] = unit_kick2(q, h, "VVSVSV"[q * GF + h])
-        for h in range(GF):
-            units["G%d" % h] = unit_gain(h)
-        units["Za"] = unit_kick2(2, 1, "V", 0, 1)
-        units["Zb"] = unit_kick2(2, 1, "V", 1, 1)
-        steps = [
-            [units["K00"], units["A10"], units["E01"]],
-            [units["A11"], units["X10"], units["X11"], units["X12"]],
-            [units["A12"], units["E10"], units["E11"]],
-            [units["X20"], units["X21"], units["X22"]],
-            [units["K10"], units["E20"], units["E21"]],
-            [units["K01"]],
-            [units["K11"]],
-            [units["K20"], units["C00"]],
-            [units["K21"], units["C01"]],
-            [units["D00"], units["D01"], units["C02"]],
-            [units["D02"], units["G0"]],
-            [units["D10"], units["D11"], units["C10"]],
-            [units["D12"], units["D20"], units["C11"]],
-            [units["Y00"], units["C12"]],
-            [units["D21"], units["D22"], units["G1"]],
-            [units["Y10"]],
-            [units["Y01"]],
-            [units["Y20"]],
-            [units["Y11"]],
-            [units["Za"]],
-            [units["Zb"]],
-        ]
+        kicks = [(q, h) for h in range(GF) for q in range(PAIRS)]
+        drifts = [(q, g) for q in range(PAIRS) for g in range(GD)]
+        first_drift_row = LEAD + len(kicks) - 1
+        second_kick_row = first_drift_row + (len(drifts) + 1) // 2
+        steps = [[] for row in range(second_kick_row + len(kicks) + 1)]
 
-        def run(stage, step):
-            if 0 <= step < len(steps):
-                for unit in steps[step]:
+        steps[0].append(unit_first_kick(*kicks[0]))
+        for g in range(GD):
+            steps[g].append(unit_a(1, g, PACK * KP if g == 0 else 0))
+        for n, (q, h) in enumerate(kicks[1:]):
+            steps[LEAD + n].append(unit_first_kick(q, h))
+            if h == 0:
+                steps[n].extend(unit_x(q, g) for g in range(GD))
+            steps[n].append(unit_d(q, h))
+
+        for n, (q, g) in enumerate(drifts):
+            steps[first_drift_row + n // 2].append(unit_drift(q, g))
+
+        needs = []
+        for h in range(GF):
+            needs.extend(unit_c(h, g, VECTOR if (h, g) == (0, 0) else SCALAR) for g in range(GD))
+            needs.append(unit_gain(h))
+        for n, unit in enumerate(needs):
+            steps[second_kick_row - len(needs) + n].append(unit)
+
+        for n, (q, h) in enumerate(kicks[:-1]):
+            steps[second_kick_row + n].append(unit_second_kick(q, h, SCALAR if n % 2 else VECTOR, 0, 2))
+        for i in range(2):
+            steps[i - 2].append(unit_second_kick(*kicks[-1], VECTOR, i, 1))
+
+        def run(stage, row):
+            if 0 <= row < len(steps):
+                for unit in steps[row]:
                     if stage in unit:
                         unit[stage]()
 
@@ -423,48 +425,61 @@ def tile_linear_leapfrog_difference_b9_kernel(
             nc.gpsimd.memset(a_scale_flat[BLOCKS:P, :], 0.0)
             make_identity(nc, ident[:])
             nc.gpsimd.memset(b_scale[:].rearrange("p g n -> p (g n)").bitcast(I32), 0)
+
             load_a(0, 0)
-            scale_rows = A_scale.rearrange("a (b o) -> (a b) o", o=1)
-            nc.sync.dma_start(out=a_scale_flat[0:64, :], in_=scale_rows[0:64, :])
-            nc.sync.dma_start(out=a_scale_flat[64:BLOCKS, :], in_=scale_rows[64:BLOCKS, :])
+            load_a_scale()
             load_a(0, 1)
             load_x(0)
             load_a(0, 2)
             load_a(1, 0)
             load_d(0)
-            load_cols()
+            load_stride_gain()
             load_a(1, 1)
             load_a(1, 2)
-            load_x(1)
-            load_d(1)
-            load_x(2)
-            load_d(2)
+            for q in range(1, PAIRS):
+                load_x(q)
+                load_d(q)
             load_c(0)
             load_b()
-            load_c(1)
-            load_c(2)
+            for g in range(1, GD):
+                load_c(g)
 
             spread = bank("sum")
             nc.tensor.transpose(spread[:, 0:P], a_scale_flat[:].to_broadcast([P, P]), ident[:])
-            by_row = spread[:, 0:BLOCKS].rearrange("p (g q b) -> p g q b", g=GD, q=4)
-            for quad in range(4):
+            by_row = spread[:, 0:BLOCKS].rearrange("p (g r b) -> p g r b", g=GD, r=QUADS)
+            for quad in range(QUADS):
                 part = slice(32 * quad, 32 * quad + 32)
                 nc.scalar.activation(out=a_scale[part], in_=by_row[part, :, quad, :], func=COPY)
-            for name, stage in [("A00", "drain"), ("A01", "drain"), ("A00", "group"), ("A02", "drain"), ("A01", "group"), ("A00", "quant"), ("X00", "turn"), ("X01", "turn"), ("X02", "turn"), ("E00", "turn"), ("X00", "drain"), ("X01", "drain"), ("X02", "drain"), ("E00", "drain"), ("A01", "quant"), ("A02", "group"), ("X00", "quant"), ("X01", "quant"), ("A02", "quant"), ("X02", "quant"), ("cols", "group")]:
-                units[name][stage]()
+
+            head_a = [unit_a(0, g, SPLIT if g == 0 else 0) for g in range(GD)]
+            head_x = [unit_x(0, g) for g in range(GD)]
+            head_turns = head_x + [unit_d(0, 0)]
+            for unit in head_a:
+                unit["drain"]()
+            for stage in ("turn", "drain"):
+                for unit in head_turns:
+                    unit[stage]()
+            for unit in head_a[:-1]:
+                unit["group"]()
+                unit["quant"]()
+            head_a[-1]["group"]()
+            for unit in head_x + head_a[-1:]:
+                unit["quant"]()
+            nc.vector.tensor_copy(out=stride_col[:], in_=stride_raw[:])
+            nc.vector.tensor_copy(out=gain_col[:], in_=gain_raw[:])
 
         with tc.manual_schedule(engines={mybir.EngineType.PE}):
             run("matmul", 0)
             run("matmul", 1)
-            for s in range(len(steps) + 1):
-                run("group", s - 1)
-                run("add", s)
-                run("turn", s)
-                run("drain", s)
-                run("quant", s - 1)
-                run("matmul", s + 2)
+            for row in range(len(steps) + 1):
+                run("group", row - 1)
+                run("add", row)
+                run("turn", row)
+                run("drain", row)
+                run("quant", row - 1)
+                run("matmul", row + 2)
 
-        for quad in range(4):
+        for quad in range(QUADS):
             (nc.sync if quad % 2 else nc.scalar).dma_start(
                 out=out_2[:, 4 * quad : 4 * quad + 4, :].rearrange("g r m -> r g m").bitcast(I32),
                 in_=y_scales[32 * quad : 32 * quad + 4, :, :].bitcast(I32),

from contextlib import ExitStack

import concourse.mybir as mybir
from concourse.masks import make_identity

T, D, F = 768, 1536, 1024
FLOPS = 2 * T * D * F * 3

F32 = mybir.dt.float32
BF16 = mybir.dt.bfloat16
U32 = mybir.dt.uint32
I32 = mybir.dt.int32
U8 = mybir.dt.uint8
FP8 = mybir.dt.float8_e4m3fn
FP8X4 = mybir.dt.float8_e4m3fn_x4
FP4X4 = mybir.dt.float4_e2m1fn_x4
ALU = mybir.AluOpType
COPY = mybir.ActivationFunctionType.Copy
VECTOR, SCALAR = "vector", "scalar"

P = 128
PACK = 4
KP = P * PACK
GD = D // KP
GF = F // KP
PAIR = 2 * P
PAIRS = T // PAIR
BLK = 128
BLOCKS = (D // BLK) * (F // BLK)
QUADS = 4
SPLIT = 1280
LEAD = 3


def tile_linear_leapfrog_difference_b9_kernel(
    tc, x, d, A_bytes, A_scale, B_words, B_scales, C, stride, gain, out_0, out_1, out_2
):
    nc = tc.nc
    with ExitStack() as ctx:
        keep = ctx.enter_context(tc.tile_pool(name="keep", bufs=1))
        work = ctx.enter_context(tc.tile_pool(name="work", bufs=3))
        psum = ctx.enter_context(tc.psum_pool(name="psum", bufs=8))

        def kept(name, shape, dtype):
            return keep.tile(shape, dtype, name=name, align_bytes=64)

        def staged(name, shape, dtype, bufs):
            return work.tile(shape, dtype, name=name, tag=name, bufs=bufs, align_bytes=64)

        def bank(role):
            return psum.tile([P, KP], F32, name=role, tag="bank")

        ident = kept("ident", [P, P], F32)
        a_scale_flat = kept("a_scale_flat", [P, 1], F32)
        a_scale = kept("a_scale", [P, GD, F // BLK], F32)
        b_words = kept("b_words", [P, GF, 2 * D], U8)
        b_scale = kept("b_scale", [P, GF, D], U8)
        stride_raw = kept("stride_raw", [P, GF, PACK], BF16)
        gain_raw = kept("gain_raw", [P, GF, PACK], BF16)
        stride_col = kept("stride_col", [P, GF, PACK], F32)
        gain_col = kept("gain_col", [P, GF, PACK], F32)
        e = [kept("e_%d" % h, [P, PACK, T], F32) for h in range(GF)]
        y_scales = kept("y_scales", [P, GF, T], U8)
        words_out = out_1.rearrange("g p m t -> g p (m t)").bitcast(I32)

        a_raw, c_raw, x_sb, d_sb = {}, {}, {}, {}
        a_codes, a_scales, c_codes, c_scales = {}, {}, {}, {}
        x_codes, x_scales, x1_codes, x1_scales = {}, {}, {}, {}
        u_codes, u_scales, y_codes, d_turned = {}, {}, {}, {}


        def load_a(h, g):
            a_raw[h, g] = kept("a_bytes_%d_%d" % (h, g), [P, PACK, KP], U8)
            rows = A_bytes[g * KP : (g + 1) * KP, h * KP : (h + 1) * KP]
            nc.sync.dma_start(out=a_raw[h, g][:], in_=rows.rearrange("(p j) f -> p j f", j=PACK))

        def load_a_scale():
            flat = A_scale.rearrange("a (b o) -> (a b) o", o=1)
            nc.sync.dma_start(out=a_scale_flat[0:64, :], in_=flat[0:64, :])
            nc.sync.dma_start(out=a_scale_flat[64:BLOCKS, :], in_=flat[64:BLOCKS, :])

        def load_c(g):
            c_raw[g] = kept("c_raw_%d" % g, [P, PACK, F], BF16)
            rows = C[g * KP : (g + 1) * KP, :]
            nc.sync.dma_start(out=c_raw[g][:], in_=rows.rearrange("(p j) f -> p j f", j=PACK))

        def load_x(q):
            x_sb[q] = kept("x_%d" % q, [P, 2, D], BF16)
            rows = x[q * PAIR : (q + 1) * PAIR, :]
            nc.sync.dma_start(out=x_sb[q][:], in_=rows.rearrange("(i p) k -> p i k", p=P))

        def load_d(q):
            d_sb[q] = kept("d_%d" % q, [P, 2, F], BF16)
            rows = d[q * PAIR : (q + 1) * PAIR, :]
            nc.sync.dma_start(out=d_sb[q][:], in_=rows.rearrange("(i p) f -> p i f", p=P))

        def load_stride_gain():
            nc.sync.dma_start(out=stride_raw[:], in_=stride.rearrange("o (g p t) -> p (o g) t", p=P, t=PACK))
            nc.sync.dma_start(out=gain_raw[:], in_=gain.rearrange("o (g p t) -> p (o g) t", p=P, t=PACK))

        def load_b():
            for quad in range(QUADS):
                nc.sync.dma_start(
                    out=b_scale[32 * quad : 32 * quad + 4, :, :].bitcast(I32),
                    in_=B_scales[:, 4 * quad : 4 * quad + 4, :].rearrange("g r n -> r g n").bitcast(I32),
                )
            nc.sync.dma_start(
                out=b_words[:].bitcast(I32), in_=B_words.rearrange("g p n -> p g n").bitcast(I32)
            )


        def copy_on(engine, out, in_):
            if engine == VECTOR:
                nc.vector.tensor_copy(out=out, in_=in_)
            else:
                nc.scalar.copy(out=out, in_=in_)

        def interleave(engine, grouped, slices):
            copy_on(
                engine,
                grouped[:].rearrange("p (c i) t -> p c t i", i=PACK),
                slices[:].rearrange("p t (c i) -> p c t i", i=PACK),
            )

        def quantize(codes, scales, grouped):
            nc.vector.quantize_mx(out=codes.bitcast(FP8X4), scales=scales, in_=grouped)

        def quantize_into(name, codes, scales, key, grouped, bufs):
            width = grouped.shape[1] // PACK
            codes[key] = staged(name + "_codes", [P, width], U32, bufs)
            scales[key] = staged(name + "_scales", [P, width], U8, bufs)
            quantize(codes[key][:], scales[key][:], grouped)

        def turn_words(st, words):
            st["ps"] = bank("turn")
            parts = st["ps"][:].rearrange("p (i u r) -> p i u r", i=2, u=2)
            for i in range(2):
                for u in range(2):
                    nc.tensor.transpose(parts[:, i, u, :], words(i, u), ident[:])

        def drain_words(st):
            st["grouped"] = staged("pos_grouped", [P, PAIR * PACK], BF16, 4)
            nc.scalar.copy(
                out=st["grouped"][:].bitcast(F32).rearrange("p (i r u) -> p i r u", i=2, u=2),
                in_=st["ps"][:].rearrange("p (i u r) -> p i r u", i=2, u=2),
            )

        def kick_matmuls(w_codes, w_scales, h, pos_codes, pos_scales, q, rows):
            width = rows.stop - rows.start
            sums, banks = [], []
            for t in range(PACK):
                place = t % (KP // width)
                if place == 0:
                    banks.append(bank("sum"))
                sums.append(banks[-1][:, place * width : (place + 1) * width])
                for g in range(GD):
                    nc.tensor.matmul_mx(
                        out=sums[t],
                        lhsT=w_codes[h, g][:, t * P : (t + 1) * P].bitcast(FP8X4),
                        lhsT_scale=w_scales[h, g][:, t * P : (t + 1) * P],
                        rhs=pos_codes[q, g][:, rows].bitcast(FP8X4),
                        rhs_scale=pos_scales[q, g][:, rows],
                        start=(g == 0),
                        stop=(g == GD - 1),
                    )
            return sums, banks


        def unit_a(h, g, vector_cols):
            st = {}

            def widen():
                st["wide"] = staged("a_wide", [P, PACK, KP], BF16, 3)
                dst = st["wide"][:].rearrange("p j f -> p (j f)")
                src = a_raw[h, g][:].rearrange("p j f -> p (j f)").bitcast(FP8)
                if vector_cols > 0:
                    nc.vector.tensor_copy(out=dst[:, :vector_cols], in_=src[:, :vector_cols])
                if vector_cols < PACK * KP:
                    nc.scalar.copy(out=dst[:, vector_cols:], in_=src[:, vector_cols:])

            def group():
                st["grouped"] = staged("w_grouped", [P, PACK, P, PACK], BF16, 3)
                src = st["wide"][:].rearrange("p j (m t) -> p m j t", t=PACK)
                dst = st["grouped"][:].rearrange("p t m j -> p m j t")
                for b in range(KP // BLK):
                    ms = slice(32 * b, 32 * b + 32)
                    col = h * (KP // BLK) + b
                    nc.vector.tensor_scalar(
                        out=dst[:, ms], in0=src[:, ms],
                        scalar1=a_scale[:, g, col : col + 1], scalar2=None, op0=ALU.mult,
                    )

            def quant():
                grouped = st["grouped"][:].rearrange("p t m j -> p (t m j)")
                quantize_into("a", a_codes, a_scales, (h, g), grouped, GF * GD)

            return {"drain": widen, "group": group, "quant": quant}

        def unit_c(h, g, engine):
            st = {}

            def group():
                st["grouped"] = staged("w_grouped", [P, PACK, P, PACK], BF16, 3)
                copy_on(
                    engine,
                    st["grouped"][:].rearrange("p t m j -> p m j t"),
                    c_raw[g][:, :, h * KP : (h + 1) * KP].rearrange("p j (m t) -> p m j t", t=PACK),
                )

            def quant():
                grouped = st["grouped"][:].rearrange("p t m j -> p (t m j)")
                quantize_into("c", c_codes, c_scales, (h, g), grouped, GF * GD)

            return {"group" if engine == VECTOR else "drain": group, "quant": quant}

        def unit_x(q, g):
            st = {}

            def words(i, u):
                return x_sb[q][:].bitcast(F32)[:, i, 256 * g + u : 256 * (g + 1) : 2]

            return {
                "turn": lambda: turn_words(st, words),
                "drain": lambda: drain_words(st),
                "quant": lambda: quantize_into("pos", x_codes, x_scales, (q, g), st["grouped"][:], 12),
            }

        def unit_d(q, h):
            st = {}

            def turn():
                words = d_sb[q][:].bitcast(F32)
                st["ps"] = bank("turn")
                parts = st["ps"][:].rearrange("p (u i r) -> p u i r", i=2, u=2)
                for u in range(2):
                    for i in range(2):
                        nc.tensor.transpose(
                            parts[:, u, i, :], words[:, i, 256 * h + u : 256 * (h + 1) : 2], ident[:]
                        )

            def drain():
                d_turned[q, h] = staged("d_turned", [P, KP], F32, 4)
                nc.scalar.copy(out=d_turned[q, h][:], in_=st["ps"][:])

            return {"turn": turn, "drain": drain}

        def unit_first_kick(q, h):
            st = {}
            cols = slice(q * PAIR, (q + 1) * PAIR)

            def matmul():
                st["banks"] = kick_matmuls(a_codes, a_scales, h, x_codes, x_scales, q, slice(0, PAIR))[1]

            def add():
                halves = d_turned[q, h][:].bitcast(BF16).rearrange("p (u r s) -> p u s r", u=2, s=2)
                for u in range(2):
                    nc.vector.tensor_tensor(
                        out=e[h][:, 2 * u : 2 * u + 2, cols],
                        in0=st["banks"][u][:].rearrange("p (s r) -> p s r", s=2),
                        in1=halves[:, u],
                        op=ALU.add,
                    )

            def drain():
                st["slices"] = staged("u_slices", [P, PACK, PAIR], BF16, 2)
                for t in range(PACK):
                    nc.scalar.activation(
                        out=st["slices"][:, t, :], in_=e[h][:, t, cols], func=COPY,
                        scale=stride_col[:, h, t : t + 1],
                    )

            def group():
                st["grouped"] = staged("mode_grouped", [P, PAIR, PACK], BF16, 3)
                interleave(VECTOR, st["grouped"], st["slices"])

            def quant():
                grouped = st["grouped"][:].rearrange("p r t -> p (r t)")
                quantize_into("u", u_codes, u_scales, (q, h), grouped, PAIRS * GF)

            return {"matmul": matmul, "add": add, "drain": drain, "group": group, "quant": quant}

        def unit_drift(q, g):
            st = {}

            def matmul():
                st["banks"] = []
                for i in range(2):
                    st["banks"].append(bank("sum"))
                    cols = slice(i * P, (i + 1) * P)
                    for h in range(GF):
                        nc.tensor.matmul_mx(
                            out=st["banks"][i][:],
                            lhsT=u_codes[q, h][:, cols].bitcast(FP8X4),
                            lhsT_scale=u_scales[q, h][:, cols],
                            rhs=b_words[:, h, 2 * KP * g : 2 * KP * (g + 1)].bitcast(FP4X4),
                            rhs_scale=b_scale[:, h, KP * g : KP * (g + 1)],
                            start=(h == 0),
                            stop=(h == GF - 1),
                        )

            def add():
                st["x1"] = staged("x1", [P, 2, KP], BF16, 2)
                for i in range(2):
                    nc.vector.tensor_tensor(
                        out=st["x1"][:, i, :].rearrange("p (u m s) -> p u m s", u=2, s=2),
                        in0=st["banks"][i][:].rearrange("p (m u s) -> p u m s", u=2, s=2),
                        in1=x_sb[q][:, i, g * KP : (g + 1) * KP].rearrange("p (m u s) -> p u m s", u=2, s=2),
                        op=ALU.add,
                    )

            def words(i, u):
                return st["x1"][:].bitcast(F32)[:, i, u * P : (u + 1) * P]

            return {
                "matmul": matmul,
                "add": add,
                "turn": lambda: turn_words(st, words),
                "drain": lambda: drain_words(st),
                "quant": lambda: quantize_into("pos", x1_codes, x1_scales, (q, g), st["grouped"][:], 12),
            }

        def unit_gain(h):
            def drain():
                for t in range(PACK):
                    nc.scalar.activation(
                        out=e[h][:, t, :], in_=e[h][:, t, :], func=COPY, scale=gain_col[:, h, t : t + 1]
                    )

            return {"drain": drain}

        def unit_second_kick(q, h, engine, first, tiles):
            st = {}
            width = tiles * P
            rows = slice(first * P, first * P + width)
            cols = slice(q * PAIR + rows.start, q * PAIR + rows.stop)

            def matmul():
                st["sums"] = kick_matmuls(c_codes, c_scales, h, x1_codes, x1_scales, q, rows)[0]

            def add():
                st["y"] = staged("y_turned", [P, PACK, width], F32, 3)
                for t in range(PACK):
                    nc.vector.scalar_tensor_tensor(
                        out=st["y"][:, t, :], in0=st["sums"][t],
                        scalar=gain_col[:, h, t : t + 1], in1=e[h][:, t, cols],
                        op0=ALU.mult, op1=ALU.add,
                    )

            def turn():
                st["banks"] = []
                for i in range(tiles):
                    st["banks"].append(bank("turn"))
                    for t in range(PACK):
                        nc.tensor.transpose(
                            st["banks"][i][:, t * P : (t + 1) * P], st["y"][:, t, i * P : (i + 1) * P], ident[:]
                        )

            def group():
                st["grouped"] = staged("mode_grouped", [P, width, PACK], BF16, 3)
                interleave(engine, st["grouped"], st["y"])

            def drain():
                if engine == SCALAR:
                    group()
                y_rows = staged("y_rows", [P, tiles, P, PACK], F32, 3)
                for i in range(tiles):
                    nc.scalar.copy(out=y_rows[:, i], in_=st["banks"][i][:].rearrange("r (t m) -> r m t", t=PACK))
                nc.sync.dma_start(
                    out=out_0[cols, h * KP : (h + 1) * KP].rearrange("(i r) f -> r i f", r=P),
                    in_=y_rows[:].rearrange("r i m t -> r i (m t)"),
                )

            def quant():
                if first == 0:
                    y_codes[q, h] = staged("y_codes", [P, PAIR], U32, 3)
                grouped = st["grouped"][:].rearrange("p r t -> p (r t)")
                quantize(y_codes[q, h][:, rows], y_scales[:, h, cols], grouped)
                if rows.stop == PAIR:
                    nc.sync.dma_start(
                        out=words_out[h, :, q * PAIR : (q + 1) * PAIR], in_=y_codes[q, h][:].bitcast(I32)
                    )

            stages = {"matmul": matmul, "add": add, "turn": turn, "drain": drain, "quant": quant}
            if engine == VECTOR:
                stages["group"] = group
            return stages

        kicks = [(q, h) for h in range(GF) for q in range(PAIRS)]
        drifts = [(q, g) for q in range(PAIRS) for g in range(GD)]
        first_drift_row = LEAD + len(kicks) - 1
        second_kick_row = first_drift_row + (len(drifts) + 1) // 2
        steps = [[] for row in range(second_kick_row + len(kicks) + 1)]

        steps[0].append(unit_first_kick(*kicks[0]))
        for g in range(GD):
            steps[g].append(unit_a(1, g, PACK * KP if g == 0 else 0))
        for n, (q, h) in enumerate(kicks[1:]):
            steps[LEAD + n].append(unit_first_kick(q, h))
            if h == 0:
                steps[n].extend(unit_x(q, g) for g in range(GD))
            steps[n].append(unit_d(q, h))

        for n, (q, g) in enumerate(drifts):
            steps[first_drift_row + n // 2].append(unit_drift(q, g))

        needs = []
        for h in range(GF):
            needs.extend(unit_c(h, g, VECTOR if (h, g) == (0, 0) else SCALAR) for g in range(GD))
            needs.append(unit_gain(h))
        for n, unit in enumerate(needs):
            steps[second_kick_row - len(needs) + n].append(unit)

        for n, (q, h) in enumerate(kicks[:-1]):
            steps[second_kick_row + n].append(unit_second_kick(q, h, SCALAR if n % 2 else VECTOR, 0, 2))
        for i in range(2):
            steps[i - 2].append(unit_second_kick(*kicks[-1], VECTOR, i, 1))

        def run(stage, row):
            if 0 <= row < len(steps):
                for unit in steps[row]:
                    if stage in unit:
                        unit[stage]()

        with tc.manual_schedule():
            nc.gpsimd.memset(a_scale_flat[BLOCKS:P, :], 0.0)
            make_identity(nc, ident[:])
            nc.gpsimd.memset(b_scale[:].rearrange("p g n -> p (g n)").bitcast(I32), 0)

            load_a(0, 0)
            load_a_scale()
            load_a(0, 1)
            load_x(0)
            load_a(0, 2)
            load_a(1, 0)
            load_d(0)
            load_stride_gain()
            load_a(1, 1)
            load_a(1, 2)
            for q in range(1, PAIRS):
                load_x(q)
                load_d(q)
            load_c(0)
            load_b()
            for g in range(1, GD):
                load_c(g)

            spread = bank("sum")
            nc.tensor.transpose(spread[:, 0:P], a_scale_flat[:].to_broadcast([P, P]), ident[:])
            by_row = spread[:, 0:BLOCKS].rearrange("p (g r b) -> p g r b", g=GD, r=QUADS)
            for quad in range(QUADS):
                part = slice(32 * quad, 32 * quad + 32)
                nc.scalar.activation(out=a_scale[part], in_=by_row[part, :, quad, :], func=COPY)

            head_a = [unit_a(0, g, SPLIT if g == 0 else 0) for g in range(GD)]
            head_x = [unit_x(0, g) for g in range(GD)]
            head_turns = head_x + [unit_d(0, 0)]
            for unit in head_a:
                unit["drain"]()
            for stage in ("turn", "drain"):
                for unit in head_turns:
                    unit[stage]()
            for unit in head_a[:-1]:
                unit["group"]()
                unit["quant"]()
            head_a[-1]["group"]()
            for unit in head_x + head_a[-1:]:
                unit["quant"]()
            nc.vector.tensor_copy(out=stride_col[:], in_=stride_raw[:])
            nc.vector.tensor_copy(out=gain_col[:], in_=gain_raw[:])

        with tc.manual_schedule(engines={mybir.EngineType.PE}):
            run("matmul", 0)
            run("matmul", 1)
            for row in range(len(steps) + 1):
                run("group", row - 1)
                run("add", row)
                run("turn", row)
                run("drain", row)
                run("quant", row - 1)
                run("matmul", row + 2)

        for quad in range(QUADS):
            (nc.sync if quad % 2 else nc.scalar).dma_start(
                out=out_2[:, 4 * quad : 4 * quad + 4, :].rearrange("g r m -> r g m").bitcast(I32),
                in_=y_scales[32 * quad : 32 * quad + 4, :, :].bitcast(I32),
            )
